import numpy as np, ml_dtypes
CORES = [66,74,82,90,194,202,210,218]
N = 8
import mx_ref
BF = ml_dtypes.bfloat16
def cols(t, e):
    v = np.concatenate([t.reshape(128, -1, 4), np.zeros((128, 1, 4), BF)], axis=1)
    return np.ascontiguousarray(v[:, e]).reshape(128, -1)
def f(rng, *shape):
    return mx_ref.flush((rng.standard_normal(shape, dtype=np.float32) * np.exp2(rng.integers(-2, 3, shape[:-1] + (1,)))).astype(BF))
def wide(rng, *shape, cols=0):
    v = rng.standard_normal(shape, dtype=np.float32) * np.exp2(rng.integers(-12, 13, shape)).astype(np.float32)
    if cols: v *= np.repeat(np.exp2(rng.integers(-cols, cols + 1, shape[:-2] + (1, shape[-1] // 4))) * (rng.random(shape[:-2] + (1, shape[-1] // 4)) > 0.0625), 4, axis=-1).astype(np.float32)
    return mx_ref.flush(v.astype(BF))
T, G, C = 256, 8, 16
def lean(rng, d, sizes):
    p, t = rng.integers(0, 128), rng.integers(0, 4)
    q, v = np.array(d["qw"]), np.array(d["x"])
    q[:, p, t::4] = BF(128)
    v[:, p, t::4] = np.repeat(np.asarray(sizes, np.float32), 16).astype(BF)
    return {"qw": q, "x": v}
def setup_inputs(rng):
    return {"qw": f(rng, N, 128, 512), "x": f(rng, N, 128, 4 * T)}
def setup_inputs_ties(rng):
    d = setup_inputs(rng); v = []
    for s in range(N):
        k = rng.permutation(np.arange(C) // 4)
        v.append(cols(d["x"][s], np.concatenate([16 * c + rng.permutation(16) for c in k])))
    d["x"] = np.stack(v); return d
def setup_inputs_last(rng):
    return lean(rng, setup_inputs(rng), [0] * (C - 1) + [128])
def setup_inputs_alike(rng):
    d = setup_inputs(rng); d["qw"] = np.concatenate([d["qw"][:, :, :64]] * G, axis=2); return d
def setup_inputs_below(rng):
    return lean(rng, setup_inputs(rng), [-128 * 4096] * C)
def setup_inputs_spread(rng):
    d = setup_inputs(rng); d["x"] = wide(rng, N, 128, 4 * T); return d
def check_inputs(d):
    b = []
    for k in ("qw", "x"):
        a = np.abs(np.asarray(d[k]).astype(np.float32))
        if not ((a == 0) | ((a >= 2.0 ** -30) & (a <= 2.0 ** 30))).all(): b.append(k)
    return b
def decode(q, n):
    out = np.zeros((128, 4 * n), np.float32)
    for b in range(4):
        e = np.zeros((128, 128, 4), np.float32); e[np.arange(128), np.arange(128), b] = 1
        out[:, b::4] = mx_ref.matmul(mx_ref.quantize(e.reshape(128, 512).astype(BF)), q)
    return out
def reference(qw, x):
    W = [mx_ref.quantize(qw[r]) for r in range(N)]
    X = [mx_ref.quantize(x[s]) for s in range(N)]
    R = [mx_ref.quantize((x[s].astype(np.float32) - decode(X[s], T)).astype(BF)) for s in range(N)]
    y = np.zeros((N, 128, N * G * 16), np.float32); ch = np.zeros((N, G, N), np.float32)
    for r in range(N):
        for s in range(N):
            a, b = mx_ref.matmul(W[r], X[s]), mx_ref.matmul(W[r], R[s])
            best = a.reshape(G, 16, C, 16).max(axis=(1, 3)).argmax(axis=1)
            ch[r][:, s] = best
            for g in range(G):
                i, j = 16 * (s * G + g), 16 * int(best[g])
                y[r][:, i:i + 16] = a[:, j:j + 16] + b[:, j:j + 16]
    return {"y": y, "ch": ch}

@@ -1,0 +1,386 @@
+from concourse.bass import DstId, RemoteDMATransfer
+from concourse.mybir import dt, AluOpType, AxisListType, ActivationFunctionType
+
+N = 8
+G = 8
+C = 16
+BIG = 1e29
+
+SCRATCH = {
+    "qwb": ("sbuf", [128, 512], "bfloat16"),
+    "xb": ("sbuf", [128, 1024], "bfloat16"),
+    "rb": ("sbuf", [128, 1024], "bfloat16"),
+    "ob": ("sbuf", [128, 528], "bfloat16"),
+    "eb": ("sbuf", [128, 528], "bfloat16"),
+    "onf": ("sbuf", [128, 128], "float32"),
+    "idn": ("sbuf", [128, 128], "float32"),
+    "p16": ("sbuf", [128, 128], "float32"),
+    "msk": ("sbuf", [128, 512], "float32"),
+    "top": ("sbuf", [128, 256], "float32"),
+    "QC": ("sbuf", [128, 128 * N], "float8_e4m3fn_x4"),
+    "QS": ("sbuf", [128, 128 * N], "uint8"),
+    "XC": ("sbuf", [128, 256], "float8_e4m3fn_x4"),
+    "XS": ("sbuf", [128, 256], "uint8"),
+    "EC": ("sbuf", [128, 512], "float8_e4m3fn_x4"),
+    "ES": ("sbuf", [128, 512], "uint8"),
+    "sc": ("sbuf", [128, 2048], "float32"),
+    "rm": ("sbuf", [128, 512], "float32"),
+    "ltb": ("sbuf", [128, 32], "float32"),
+    "cc": ("sbuf", [128, 8], "float32"),
+    "bc": ("sbuf", [128, 256], "float32"),
+    "off": ("sbuf", [128, 32 * N], "uint16"),
+    "hb": ("sbuf", [128, 1024 * N], "bfloat16"),
+    "OC": ("sbuf", [128, 256 * N], "float8_e4m3fn_x4"),
+    "OS": ("sbuf", [128, 256 * N], "uint8"),
+    "LC": ("sbuf", [128, 256 * N], "float8_e4m3fn_x4"),
+    "LS": ("sbuf", [128, 256 * N], "uint8"),
+    "HQC": ("sbuf", [128, 128], "float8_e4m3fn_x4"),
+    "HQS": ("sbuf", [128, 128], "uint8"),
+    "HXC": ("sbuf", [128, 512], "float8_e4m3fn_x4"),
+    "HXS": ("sbuf", [128, 512], "uint8"),
+    "ysb": ("sbuf", [128, 128 * N], "float32"),
+    "chrow": ("sbuf", [128, 128], "float32"),
+    "chc": ("sbuf", [128, 64], "float32"),
+    "cht": ("sbuf", [128, 64], "float32"),
+    "chf": ("sbuf", [128, 8], "float32"),
+    "chd": ("dram", [128, 1], "float32"),
+    "chland": ("dram", [N, 128, 1], "float32"),
+    "psD": ("psum", [128, 1024], "float32"),
+    "psA": ("psum", [128, 1024], "float32"),
+    "psT": ("psum", [128, 512], "float32"),
+    "psY": ("psum", [128, 1536], "float32"),
+}
+SEMAPHORES = (
+    ["lq", "lx", "mo", "mf", "mk1", "mk2", "mtop", "mch", "qq", "qx", "qe", "ge", "gi", "gp"]
+    + ["dm%d" % b for b in range(4)] + ["rs%d" % b for b in range(4)]
+    + ["sm%d%d" % (b, h) for b in range(2) for h in range(2)]
+    + ["sn%d%d" % (b, h) for b in range(2) for h in range(2)]
+    + ["tr%d%d" % (b, h) for b in range(2) for h in range(2)]
+    + [n + str(b) for n in ("rmx", "ltx", "ccx", "bcx", "ctx", "ofx") for b in range(2)]
+    + [n + str(j) for n in ("gv", "gs", "qz", "ym", "yc", "q", "d") for j in range(N)]
+    + ["yd", "chr", "chs", "chl", "chi", "chg", "cht1", "chf1", "cho", "sent", "hqc", "hqs"]
+    + [n + str(j) for n in ("hxc", "hxs") for j in range(2)]
+)
+
+
+def classes(me, T, topo):
+    cores = T.cores
+    same = [r for r in range(N) if r == me or topo.same_plane(cores[me], cores[r])]
+    return same, [r for r in range(N) if r not in same]
+
+
+def slot(me, r, T, topo):
+    same, other = classes(me, T, topo)
+    return (same + other).index(r)
+
+
+def make_plan(me, T, topo):
+    cores = T.cores
+    core = cores[me]
+    same, other = classes(me, T, topo)
+    mate = [r for r in other if topo.mates(core, cores[r])][0]
+    P = sorted([r for r in same if r != me], key=lambda r: r ^ me)
+    X = sorted([r for r in other if r != mate], key=lambda r: r ^ me)
+    relays = [c for c in topo.cores_of(core) if topo.die(c) != topo.die(core)
+              and all(topo.may_write(c, cores[x]) for x in X)]
+    return {
+        "P": P, "M": mate, "X": X, "same": same, "other": other, "relays": relays,
+        "q_relay": {X[0]: 0, X[1]: 1},
+        "x_relay": {X[0]: (0, 0), P[2]: (1, 0), X[1]: (1, 1)},
+        "order": [P[0], P[2], P[1], X[0], X[1], X[2], mate, me],
+        "yorder": [P[0], P[2], P[1], me, X[0], X[2], X[1], mate],
+    }
+
+
+def count(mask):
+    return bin(mask).count("1")
+
+
+def rank_program(g, core, T, topo):
+    me = T.rank_of(core)
+    if me is None:
+        homes = [T.rank_of(c) for c in topo.cores_of(core) if T.rank_of(c) is not None]
+        if homes:
+            relay_program(g, core, homes[0], T, topo)
+        return
+    plan = make_plan(me, T, topo)
+    P, M, X, relays = plan["P"], plan["M"], plan["X"], plan["relays"]
+    cores = T.cores
+    sem = T.sem
+    order, yorder = plan["order"], plan["yorder"]
+    sl = {r: slot(me, r, T, topo) for r in range(N)}
+    own = sl[me]
+    u8 = dt.uint8
+    Op = AluOpType
+    Copy = ActivationFunctionType.Copy
+    V, S, PE, SY = g.vector, g.scalar, g.tensor, g.sync
+
+    def qcol(t, j):
+        return t[:, 128 * j:128 * j + 128]
+
+    def xcol(t, j):
+        return t[:, 256 * j:256 * j + 256]
+
+    SY.dma_start(T.qwb[:], T.qw[:]).then_inc(sem.lq, 16)
+    S.dma_start(T.xb[:], T.x[:]).then_inc(sem.lx, 16)
+
+    V.memset(T.ob[:], 1.0).then_inc(sem.mo, 1)
+    V.memset(T.onf[:], 1.0).then_inc(sem.mf, 1)
+    V.memset(T.msk[:], BIG).then_inc(sem.mk1, 1)
+    V.memset(T.top[:], BIG).then_inc(sem.mtop, 1)
+    V.memset(T.chrow[:], 0.0).then_inc(sem.mch, 1)
+    V.memset(T.chc[:], 0.0).then_inc(sem.mch, 1)
+    V.wait_ge(sem.mk1, 1)
+    V.memset(T.msk[:, 0:512:16], -BIG).then_inc(sem.mk2, 1)
+    V.wait_ge(sem.lq, 16)
+    V.quantize_mx(qcol(T.QC, own), qcol(T.QS, own), T.qwb[:]).then_inc(sem.qq, 1)
+    V.wait_ge(sem.lx, 16)
+    V.quantize_mx(T.XC[:], T.XS[:], T.xb[:]).then_inc(sem.qx, 1)
+    V.wait_ge(sem.ge, 1)
+    for b in range(4):
+        V.quantize_mx(qcol(T.EC, b), qcol(T.ES, b), T.eb[:, 4 - b:516 - b]).then_inc(sem.qe, 1)
+    for b in range(4):
+        V.wait_ge(sem["dm%d" % b], 1)
+        k = 512 * (b % 2)
+        V.tensor_tensor(T.rb[:, b:1024:4], T.xb[:, b:1024:4], T.psD[:, k:k + 256], Op.subtract).then_inc(sem["rs%d" % b], 1)
+
+    PE.wait_ge(sem.qx, 1)
+    PE.wait_ge(sem.qe, 4)
+    for b in range(4):
+        if b >= 2:
+            PE.wait_ge(sem["rs%d" % (b - 2)], 1)
+        k = 512 * (b % 2)
+        PE.matmul_mx(T.psD[:, k:k + 256], qcol(T.EC, b), qcol(T.ES, b), T.XC[:], T.XS[:], True, True).then_inc(sem["dm%d" % b], 1)
+
+    def scores_pe(bt):
+        for r in (plan["same"], plan["other"])[bt]:
+            if r == me:
+                PE.wait_ge(sem.qq, 1)
+            else:
+                PE.wait_ge(sem["q%d" % r], 16)
+        for h in range(2):
+            PE.matmul_mx(T.psA[:, 512 * h:512 * h + 512], qcol(T.XC, h), qcol(T.XS, h),
+                         T.QC[:, 512 * bt:512 * bt + 512], T.QS[:, 512 * bt:512 * bt + 512],
+                         True, True).then_inc(sem["sm%d%d" % (bt, h)], 1)
+        if bt == 0:
+            PE.wait_ge(sem.gi, 1)
+        else:
+            PE.wait_ge(sem.ofx0, 4)
+        for h in range(2):
+            k = 1024 * bt + 512 * h
+            PE.wait_ge(sem["sn%d%d" % (bt, h)], 1)
+            PE.transpose(T.psT[:, 128 * h:128 * h + 128], T.sc[:, k + 3:k + 512:4], T.idn[:]).then_inc(sem["tr%d%d" % (bt, h)], 1)
+        PE.wait_ge(sem["bcx%d" % bt], 1)
+        PE.transpose(T.psT[:, 256:384], T.bc[:, 128 * bt:128 * bt + 128], T.idn[:]).then_inc(sem["ctx%d" % bt], 1)
+
+    def scores_v(bt):
+        if bt == 0:
+            V.wait_ge(sem.mk2, 1)
+        for h in range(2):
+            k = 1024 * bt + 512 * h
+            V.wait_ge(sem["sm%d%d" % (bt, h)], 1)
+            V.tensor_tensor_scan(T.sc[:, k:k + 512], T.msk[:], T.psA[:, 512 * h:512 * h + 512], -BIG, Op.min, Op.max).then_inc(sem["sn%d%d" % (bt, h)], 1)
+        if bt == 0:
+            V.wait_ge(sem.mtop, 1)
+        V.wait_ge(sem["tr%d0" % bt], 1)
+        V.wait_ge(sem["tr%d1" % bt], 1)
+        rm = 256 * bt
+        V.tensor_tensor_scan(T.rm[:, rm:rm + 256], T.top[:], T.psT[:, 0:256], -BIG, Op.min, Op.max).then_inc(sem["rmx%d" % bt], 1)
+        V.wait_ge(sem["rmx%d" % bt], 1)
+        lt = T.ltb[:, 16 * bt:16 * bt + 16]
+        V.tensor_scalar(lt, T.rm[:, rm + 15:rm + 256:16], T.rm[:, rm + 255:rm + 256], 64.0, Op.is_lt, Op.mult).then_inc(sem["ltx%d" % bt], 1)
+        V.wait_ge(sem["ltx%d" % bt], 1)
+        V.tensor_reduce(T.cc[:, 4 * bt:4 * bt + 1], lt, AxisListType.X, Op.add).then_inc(sem["ccx%d" % bt], 1)
+        V.wait_ge(sem["ccx%d" % bt], 1)
+        if bt == 0:
+            V.wait_ge(sem.gp, 1)
+        V.tensor_scalar(T.bc[:, 128 * bt:128 * bt + 128], T.p16[:], T.cc[:, 4 * bt:4 * bt + 1], None, Op.add).then_inc(sem["bcx%d" % bt], 1)
+        V.wait_ge(sem["ctx%d" % bt], 1)
+        for e in range(4):
+            V.tensor_scalar(T.off[:, 128 * bt + e:128 * bt + 128:4], T.psT[:, 259:384:4], 16.0 * e, None, Op.add).then_inc(sem["ofx%d" % bt], 1)
+
+    def gather_s(r):
+        j = sl[r]
+        S.activation(T.hb[:, 1024 * j + 512:1024 * j + 1024], T.rb[:, 0:1024].indirect(T.off[:, 32 * j:32 * j + 32]), Copy).then_inc(sem["gs%d" % j], 1)
+
+    def gather_v(r):
+        j = sl[r]
+        V.tensor_copy(T.hb[:, 1024 * j:1024 * j + 512], T.xb[:, 0:1024].indirect(T.off[:, 32 * j:32 * j + 32])).then_inc(sem["gv%d" % j], 1)
+        V.wait_ge(sem["gv%d" % j], 1)
+        V.wait_ge(sem["gs%d" % j], 1)
+        V.quantize_mx(xcol(T.OC, j), xcol(T.OS, j), T.hb[:, 1024 * j:1024 * j + 1024]).then_inc(sem["qz%d" % j], 1)
+
+    first, second = order[:3], order[3:]
+
+    scores_pe(0)
+    scores_pe(1)
+
+    scores_v(0)
+    V.wait_ge(sem.ofx0, 4)
+    for r in first:
+        gather_v(r)
+    scores_v(1)
+    V.wait_ge(sem.ofx1, 4)
+    gather_v(second[0])
+    V.wait_ge(sem.mch, 2)
+    V.tensor_scalar(T.chrow[0:1, 0:64], T.off[0:1, 0:256:4], 1.0 / 64.0, None, Op.mult).then_inc(sem.chr, 1)
+    for r in second[1:]:
+        gather_v(r)
+
+    for b in range(4):
+        S.wait_ge(sem["rs%d" % b], 1)
+    S.wait_ge(sem.ofx0, 4)
+    for r in first:
+        gather_s(r)
+    S.wait_ge(sem.ofx1, 4)
+    for r in second:
+        gather_s(r)
+
+    sent = [0]
+
+    def tr(src, dsts, mask, rsem):
+        ids = []
+        for c, ap in dsts:
+            rid, pid = topo.addr(c, core)
+            ids.append(DstId(rid=rid, pnc=pid))
+        sent[0] += count(mask)
+        return RemoteDMATransfer(dst_ids=ids, dma_engine_mask=mask, remote_sem=rsem, srcs=[src], dsts=[ap for c, ap in dsts])
+
+    def post(*transfers):
+        g.remote_dma_fused(list(transfers), local_sem=sem.sent)
+
+    far = topo.mask(core, cores[P[0]])
+    for r in P + [M] + X:
+        far &= topo.mask(core, cores[r])
+    near = topo.mask(core, relays[0]) & topo.mask(core, relays[1]) & ~far
+
+    g.wait_ge(sem.mo, 1)
+    g.affine_select(T.eb[:], T.ob[:], [[-1, 528]], Op.is_equal, 0.0, 4, 4).then_inc(sem.ge, 1)
+
+    g.wait_ge(sem.qq, 1)
+    straight = [M] + [x for x in X if x not in plan["q_relay"]]
+    helpers = [relays[i] for i in sorted(plan["q_relay"].values())]
+
+    def qpair(buf, ranks):
+        out = []
+        for r in ranks:
+            v = qcol(T[buf], slot(r, me, T, topo))
+            out.append((cores[r], v.bitcast(u8) if buf == "QC" else v))
+        return out
+
+    qsem = sem["q%d" % me]
+    post(tr(qcol(T.QC, own).bitcast(u8), qpair("QC", P), far, qsem),
+         tr(qcol(T.QC, own).bitcast(u8), [(c, T.HQC[:].bitcast(u8)) for c in helpers], near, sem.hqc))
+    post(tr(qcol(T.QS, own), qpair("QS", P), far, qsem),
+         tr(qcol(T.QS, own), [(c, T.HQS[:]) for c in helpers], near, sem.hqs))
+    post(tr(qcol(T.QC, own).bitcast(u8), qpair("QC", straight), far, qsem))
+    post(tr(qcol(T.QS, own), qpair("QS", straight), far, qsem))
+
+    g.wait_ge(sem.mf, 1)
+    g.affine_select(T.idn[:], T.onf[:], [[-1, 128]], Op.is_equal, 0.0, 0, 1).then_inc(sem.gi, 1)
+    g.iota(T.p16[:], [[0, 8], [1, 16]], 0, 0, allow_small_or_imprecise_dtypes=True).then_inc(sem.gp, 1)
+
+    dsem = sem["d%d" % me]
+
+    def chosen(ranks):
+        for r in ranks:
+            g.wait_ge(sem["qz%d" % sl[r]], 1)
+        codes, planes = [], []
+        for r in ranks:
+            j, k = sl[r], slot(r, me, T, topo)
+            if r in plan["x_relay"]:
+                i, n = plan["x_relay"][r]
+                codes.append(tr(xcol(T.OC, j).bitcast(u8), [(relays[i], xcol(T.HXC, n).bitcast(u8))], near, sem["hxc%d" % n]))
+                planes.append(tr(xcol(T.OS, j), [(relays[i], xcol(T.HXS, n))], near, sem["hxs%d" % n]))
+            else:
+                codes.append(tr(xcol(T.OC, j).bitcast(u8), [(cores[r], xcol(T.LC, k).bitcast(u8))], far, dsem))
+                planes.append(tr(xcol(T.OS, j), [(cores[r], xcol(T.LS, k))], far, dsem))
+        post(*codes)
+        post(*planes)
+
+    chosen([P[0], P[2]])
+    chosen([P[1]])
+    chosen([X[0]])
+    chosen([X[1], X[2]])
+    one = 1 << topo.engines(core, cores[M])[0]
+    g.wait_ge(sem.chs, 16)
+    post(tr(T.chd[:], [(cores[r], T.chland[slot(r, me, T, topo)]) for r in P + [M] + X], one, sem.chi))
+    chosen([M])
+    g.wait_ge(sem.sent, sent[0])
+
+    for i, s in enumerate(yorder):
+        j, k = sl[s], 512 * (i % 3)
+        if s == me:
+            PE.wait_ge(sem["qz%d" % j], 1)
+            cod, sca = T.OC, T.OS
+        else:
+            PE.wait_ge(sem["d%d" % s], 16)
+            cod, sca = T.LC, T.LS
+        if i >= 3:
+            PE.wait_ge(sem["yc%d" % sl[yorder[i - 3]]], 1)
+        for part in range(2):
+            a = 256 * j + 128 * part
+            mm = PE.matmul_mx(T.psY[:, k:k + 128], qcol(T.QC, own), qcol(T.QS, own),
+                              cod[:, a:a + 128], sca[:, a:a + 128], part == 0, part == 1)
+        mm.then_inc(sem["ym%d" % j], 1)
+        S.wait_ge(sem["ym%d" % j], 1)
+        S.activation(T.ysb[:, 128 * s:128 * s + 128], T.psY[:, k:k + 128], Copy).then_inc(sem["yc%d" % j], 1)
+        S.wait_ge(sem["yc%d" % j], 1)
+        S.dma_start(T.y[:, 128 * s:128 * s + 128], T.ysb[:, 128 * s:128 * s + 128]).then_inc(sem.yd, 16)
+    S.wait_ge(sem.yd, 16 * N)
+
+    SY.wait_ge(sem.chr, 1)
+    SY.dma_start(T.chd[:], T.chrow[0:1, :]).then_inc(sem.chs, 16)
+    SY.dma_start(T.chland[own], T.chrow[0:1, :]).then_inc(sem.chl, 16)
+    SY.wait_ge(sem.chl, 16)
+    SY.wait_ge(sem.chi, N - 1)
+    SY.wait_ge(sem.mch, 2)
+    i = plan["same"].index(me)
+    half = len(plan["same"])
+    SY.dma_start(T.chc[0:half, 0:8], T.chland[0:half, 8 * i:8 * i + 8, 0]).then_inc(sem.chg, 16)
+    c0 = 8 * half + 8 * i
+    SY.dma_start(T.chc[0:N - half, 32:40], T.chland[half:N, c0:c0 + 8, 0]).then_inc(sem.chg, 16)
+    V.wait_ge(sem.chg, 32)
+    V.transpose(T.cht[0:32, :], T.chc[0:32, :]).then_inc(sem.cht1, 1)
+    V.wait_ge(sem.cht1, 1)
+    for n, cl in enumerate((plan["same"], plan["other"])):
+        V.tensor_copy(T.chf[0:8, cl[0]:cl[-1] + 1:cl[1] - cl[0]], T.cht[0:8, 32 * n:32 * n + len(cl)]).then_inc(sem.chf1, 1)
+    SY.wait_ge(sem.chf1, 2)
+    SY.dma_start(T.ch[:], T.chf[0:8, :]).then_inc(sem.cho, 16)
+    SY.wait_ge(sem.cho, 16)
+
+
+def relay_program(g, core, me, T, topo):
+    plan = make_plan(me, T, topo)
+    if core not in plan["relays"][:2]:
+        return
+    cores, sem = T.cores, T.sem
+    which = plan["relays"].index(core)
+    home = cores[me]
+    near = topo.mask(home, core) & ~topo.mask(home, cores[plan["P"][0]])
+    arrive = count(near)
+    u8 = dt.uint8
+    sent = [0]
+
+    def send(dst, out, src, rsem):
+        rid, pid = topo.addr(dst, core)
+        mask = topo.mask(core, dst)
+        sent[0] += count(mask)
+        g.remote_dma_fused([RemoteDMATransfer(dst_ids=[DstId(rid=rid, pnc=pid)], dma_engine_mask=mask, remote_sem=rsem,
+                                              srcs=[src], dsts=[out])], local_sem=sem.sent)
+
+    for r, i in plan["q_relay"].items():
+        if i == which:
+            k = 128 * slot(r, me, T, topo)
+            g.wait_ge(sem.hqc, arrive)
+            send(cores[r], T.QC[:, k:k + 128].bitcast(u8), T.HQC[:].bitcast(u8), sem["q%d" % me])
+            g.wait_ge(sem.hqs, arrive)
+            send(cores[r], T.QS[:, k:k + 128], T.HQS[:], sem["q%d" % me])
+    jobs = sorted((n, r) for r, (i, n) in plan["x_relay"].items() if i == which)
+    for n, r in jobs:
+        k = 256 * slot(r, me, T, topo)
+        g.wait_ge(sem["hxc%d" % n], arrive)
+        send(cores[r], T.LC[:, k:k + 256].bitcast(u8), T.HXC[:, 256 * n:256 * n + 256].bitcast(u8), sem["d%d" % me])
+        g.wait_ge(sem["hxs%d" % n], arrive)
+        send(cores[r], T.LS[:, k:k + 256], T.HXS[:, 256 * n:256 * n + 256], sem["d%d" % me])
+    g.wait_ge(sem.sent, sent[0])

@@ -2,8 +2,6 @@ from concourse.bass import DstId, RemoteDMATransfer
 from concourse.mybir import dt, AluOpType, AxisListType, ActivationFunctionType
 
 N = 8
-G = 8
-C = 16
 BIG = 1e29
 
 SCRATCH = {
@@ -15,7 +13,7 @@ SCRATCH = {
     "onf": ("sbuf", [128, 128], "float32"),
     "idn": ("sbuf", [128, 128], "float32"),
     "p16": ("sbuf", [128, 128], "float32"),
-    "msk": ("sbuf", [128, 512], "float32"),
+    "msk": ("sbuf", [128, 256], "float32"),
     "top": ("sbuf", [128, 256], "float32"),
     "QC": ("sbuf", [128, 128 * N], "float8_e4m3fn_x4"),
     "QS": ("sbuf", [128, 128 * N], "uint8"),
@@ -53,8 +51,8 @@ SCRATCH = {
 SEMAPHORES = (
     ["lq", "lx", "mo", "mf", "mk1", "mk2", "mtop", "mch", "qq", "qx", "qe", "ge", "gi", "gp"]
     + ["dm%d" % b for b in range(4)] + ["rs%d" % b for b in range(4)]
-    + ["sm%d%d" % (b, h) for b in range(2) for h in range(2)]
-    + ["sn%d%d" % (b, h) for b in range(2) for h in range(2)]
+    + ["sm%d%d" % (b, h) for b in range(2) for h in range(4)]
+    + ["sn%d%d" % (b, h) for b in range(2) for h in range(4)]
     + ["tr%d%d" % (b, h) for b in range(2) for h in range(2)]
     + [n + str(b) for n in ("rmx", "ltx", "ccx", "bcx", "ctx", "ofx") for b in range(2)]
     + [n + str(j) for n in ("gv", "gs", "qz", "ym", "yc", "q", "d") for j in range(N)]
@@ -131,7 +129,7 @@ def rank_program(g, core, T, topo):
     V.memset(T.chrow[:], 0.0).then_inc(sem.mch, 1)
     V.memset(T.chc[:], 0.0).then_inc(sem.mch, 1)
     V.wait_ge(sem.mk1, 1)
-    V.memset(T.msk[:, 0:512:16], -BIG).then_inc(sem.mk2, 1)
+    V.memset(T.msk[:, 0:256:16], -BIG).then_inc(sem.mk2, 1)
     V.wait_ge(sem.lq, 16)
     V.quantize_mx(qcol(T.QC, own), qcol(T.QS, own), T.qwb[:]).then_inc(sem.qq, 1)
     V.wait_ge(sem.lx, 16)
@@ -152,34 +150,44 @@ def rank_program(g, core, T, topo):
         k = 512 * (b % 2)
         PE.matmul_mx(T.psD[:, k:k + 256], qcol(T.EC, b), qcol(T.ES, b), T.XC[:], T.XS[:], True, True).then_inc(sem["dm%d" % b], 1)
 
+    def bank(pair, h):
+        return (T.psA, T.psY)[pair][:, 512 * h:512 * h + 256]
+
     def scores_pe(bt):
-        for r in (plan["same"], plan["other"])[bt]:
-            if r == me:
-                PE.wait_ge(sem.qq, 1)
-            else:
-                PE.wait_ge(sem["q%d" % r], 16)
-        for h in range(2):
-            PE.matmul_mx(T.psA[:, 512 * h:512 * h + 512], qcol(T.XC, h), qcol(T.XS, h),
-                         T.QC[:, 512 * bt:512 * bt + 512], T.QS[:, 512 * bt:512 * bt + 512],
-                         True, True).then_inc(sem["sm%d%d" % (bt, h)], 1)
+        ranks = (plan["same"], plan["other"])[bt]
+        for pair in range(2):
+            for r in ranks[2 * pair:2 * pair + 2]:
+                if r == me:
+                    PE.wait_ge(sem.qq, 1)
+                else:
+                    PE.wait_ge(sem["q%d" % r], 16)
+            k = 512 * bt + 256 * pair
+            for h in range(2):
+                PE.matmul_mx(bank(pair, h), qcol(T.XC, h), qcol(T.XS, h), T.QC[:, k:k + 256], T.QS[:, k:k + 256],
+                             True, True).then_inc(sem["sm%d%d" % (bt, 2 * pair + h)], 1)
         if bt == 0:
             PE.wait_ge(sem.gi, 1)
         else:
             PE.wait_ge(sem.ofx0, 4)
         for h in range(2):
             k = 1024 * bt + 512 * h
-            PE.wait_ge(sem["sn%d%d" % (bt, h)], 1)
+            for pair in range(2):
+                PE.wait_ge(sem["sn%d%d" % (bt, 2 * pair + h)], 1)
             PE.transpose(T.psT[:, 128 * h:128 * h + 128], T.sc[:, k + 3:k + 512:4], T.idn[:]).then_inc(sem["tr%d%d" % (bt, h)], 1)
         PE.wait_ge(sem["bcx%d" % bt], 1)
         PE.transpose(T.psT[:, 256:384], T.bc[:, 128 * bt:128 * bt + 128], T.idn[:]).then_inc(sem["ctx%d" % bt], 1)
 
-    def scores_v(bt):
+    def groups_v(bt):
         if bt == 0:
             V.wait_ge(sem.mk2, 1)
-        for h in range(2):
-            k = 1024 * bt + 512 * h
-            V.wait_ge(sem["sm%d%d" % (bt, h)], 1)
-            V.tensor_tensor_scan(T.sc[:, k:k + 512], T.msk[:], T.psA[:, 512 * h:512 * h + 512], -BIG, Op.min, Op.max).then_inc(sem["sn%d%d" % (bt, h)], 1)
+        for pair in range(2):
+            for h in range(2):
+                k = 1024 * bt + 512 * h + 256 * pair
+                i = "%d%d" % (bt, 2 * pair + h)
+                V.wait_ge(sem["sm" + i], 1)
+                V.tensor_tensor_scan(T.sc[:, k:k + 256], T.msk[:], bank(pair, h), -BIG, Op.min, Op.max).then_inc(sem["sn" + i], 1)
+
+    def cells_v(bt):
         if bt == 0:
             V.wait_ge(sem.mtop, 1)
         V.wait_ge(sem["tr%d0" % bt], 1)
@@ -195,19 +203,28 @@ def rank_program(g, core, T, topo):
         if bt == 0:
             V.wait_ge(sem.gp, 1)
         V.tensor_scalar(T.bc[:, 128 * bt:128 * bt + 128], T.p16[:], T.cc[:, 4 * bt:4 * bt + 1], None, Op.add).then_inc(sem["bcx%d" % bt], 1)
+
+    def lists_v(bt):
         V.wait_ge(sem["ctx%d" % bt], 1)
         for e in range(4):
             V.tensor_scalar(T.off[:, 128 * bt + e:128 * bt + 128:4], T.psT[:, 259:384:4], 16.0 * e, None, Op.add).then_inc(sem["ofx%d" % bt], 1)
+        V.wait_ge(sem["ofx%d" % bt], 4)
+
+    share = {r: (14 if r in order[:3] else 28) for r in range(N)}
 
     def gather_s(r):
-        j = sl[r]
+        j, k = sl[r], share[r]
+        S.activation(T.hb[:, 1024 * j + 16 * k:1024 * j + 512], T.xb[:, 0:1024].indirect(T.off[:, 32 * j + k:32 * j + 32]), Copy).then_inc(sem["gs%d" % j], 1)
         S.activation(T.hb[:, 1024 * j + 512:1024 * j + 1024], T.rb[:, 0:1024].indirect(T.off[:, 32 * j:32 * j + 32]), Copy).then_inc(sem["gs%d" % j], 1)
 
     def gather_v(r):
+        j, k = sl[r], share[r]
+        V.tensor_copy(T.hb[:, 1024 * j:1024 * j + 16 * k], T.xb[:, 0:1024].indirect(T.off[:, 32 * j:32 * j + k])).then_inc(sem["gv%d" % j], 1)
+
+    def pack_v(r):
         j = sl[r]
-        V.tensor_copy(T.hb[:, 1024 * j:1024 * j + 512], T.xb[:, 0:1024].indirect(T.off[:, 32 * j:32 * j + 32])).then_inc(sem["gv%d" % j], 1)
         V.wait_ge(sem["gv%d" % j], 1)
-        V.wait_ge(sem["gs%d" % j], 1)
+        V.wait_ge(sem["gs%d" % j], 2)
         V.quantize_mx(xcol(T.OC, j), xcol(T.OS, j), T.hb[:, 1024 * j:1024 * j + 1024]).then_inc(sem["qz%d" % j], 1)
 
     first, second = order[:3], order[3:]
@@ -215,17 +232,25 @@ def rank_program(g, core, T, topo):
     scores_pe(0)
     scores_pe(1)
 
-    scores_v(0)
-    V.wait_ge(sem.ofx0, 4)
-    for r in first:
-        gather_v(r)
-    scores_v(1)
-    V.wait_ge(sem.ofx1, 4)
+    groups_v(0)
+    cells_v(0)
+    lists_v(0)
+    gather_v(first[0])
+    groups_v(1)
+    pack_v(first[0])
+    gather_v(first[1])
+    cells_v(1)
+    pack_v(first[1])
+    gather_v(first[2])
+    lists_v(1)
     gather_v(second[0])
+    pack_v(first[2])
     V.wait_ge(sem.mch, 2)
     V.tensor_scalar(T.chrow[0:1, 0:64], T.off[0:1, 0:256:4], 1.0 / 64.0, None, Op.mult).then_inc(sem.chr, 1)
+    pack_v(second[0])
     for r in second[1:]:
         gather_v(r)
+        pack_v(r)
 
     for b in range(4):
         S.wait_ge(sem["rs%d" % b], 1)
@@ -301,7 +326,8 @@ def rank_program(g, core, T, topo):
     chosen([P[0], P[2]])
     chosen([P[1]])
     chosen([X[0]])
-    chosen([X[1], X[2]])
+    chosen([X[1]])
+    chosen([X[2]])
     one = 1 << topo.engines(core, cores[M])[0]
     g.wait_ge(sem.chs, 16)
     post(tr(T.chd[:], [(cores[r], T.chland[slot(r, me, T, topo)]) for r in P + [M] + X], one, sem.chi))

@@ -3,6 +3,7 @@ from concourse.mybir import dt, AluOpType, AxisListType, ActivationFunctionType
 
 N = 8
 BIG = 1e29
+CODES, PLANE = "float8_e4m3fn_x4", "uint8"
 
 SCRATCH = {
     "qwb": ("sbuf", [128, 512], "bfloat16"),
@@ -13,33 +14,45 @@ SCRATCH = {
     "onf": ("sbuf", [128, 128], "float32"),
     "idn": ("sbuf", [128, 128], "float32"),
     "p16": ("sbuf", [128, 128], "float32"),
+    "pcol": ("sbuf", [128, 8], "float32"),
+    "m24": ("sbuf", [128, 24], "float32"),
+    "scol": ("sbuf", [128, 8], "float32"),
     "msk": ("sbuf", [128, 256], "float32"),
     "top": ("sbuf", [128, 256], "float32"),
-    "QC": ("sbuf", [128, 128 * N], "float8_e4m3fn_x4"),
-    "QS": ("sbuf", [128, 128 * N], "uint8"),
-    "XC": ("sbuf", [128, 256], "float8_e4m3fn_x4"),
-    "XS": ("sbuf", [128, 256], "uint8"),
-    "EC": ("sbuf", [128, 512], "float8_e4m3fn_x4"),
-    "ES": ("sbuf", [128, 512], "uint8"),
+    "QC": ("sbuf", [128, 128 * 6], CODES),
+    "QS": ("sbuf", [128, 128 * 6], PLANE),
+    "XC": ("sbuf", [128, 256], CODES),
+    "XS": ("sbuf", [128, 256], PLANE),
+    "RC": ("sbuf", [128, 256], CODES),
+    "RS": ("sbuf", [128, 256], PLANE),
+    "EC": ("sbuf", [128, 512], CODES),
+    "ES": ("sbuf", [128, 512], PLANE),
     "sc": ("sbuf", [128, 2048], "float32"),
-    "rm": ("sbuf", [128, 512], "float32"),
-    "ltb": ("sbuf", [128, 32], "float32"),
-    "cc": ("sbuf", [128, 8], "float32"),
-    "bc": ("sbuf", [128, 256], "float32"),
-    "off": ("sbuf", [128, 32 * N], "uint16"),
-    "hb": ("sbuf", [128, 1024 * N], "bfloat16"),
-    "OC": ("sbuf", [128, 256 * N], "float8_e4m3fn_x4"),
-    "OS": ("sbuf", [128, 256 * N], "uint8"),
-    "LC": ("sbuf", [128, 256 * N], "float8_e4m3fn_x4"),
-    "LS": ("sbuf", [128, 256 * N], "uint8"),
-    "HQC": ("sbuf", [128, 128], "float8_e4m3fn_x4"),
-    "HQS": ("sbuf", [128, 128], "uint8"),
-    "HXC": ("sbuf", [128, 512], "float8_e4m3fn_x4"),
-    "HXS": ("sbuf", [128, 512], "uint8"),
+    "rm": ("sbuf", [128, 768], "float32"),
+    "ltb": ("sbuf", [128, 48], "float32"),
+    "cc": ("sbuf", [128, 12], "float32"),
+    "bc": ("sbuf", [128, 384], "float32"),
+    "off": ("sbuf", [128, 32 * 6], "uint16"),
+    "offl": ("sbuf", [128, 32], "uint16"),
+    "hb": ("sbuf", [128, 1024 * 6], "bfloat16"),
+    "OC": ("sbuf", [128, 256 * 6], CODES),
+    "OS": ("sbuf", [128, 256 * 6], PLANE),
+    "LC": ("sbuf", [128, 256 * 6], CODES),
+    "LS": ("sbuf", [128, 256 * 6], PLANE),
+    "FC": ("sbuf", [128, 1024], CODES),
+    "FS": ("sbuf", [128, 1024], PLANE),
+    "HFC": ("sbuf", [128, 512], CODES),
+    "HFS": ("sbuf", [128, 512], PLANE),
+    "HXC": ("sbuf", [128, 256], CODES),
+    "HXS": ("sbuf", [128, 256], PLANE),
+    "pf": ("sbuf", [128, 768], "float32"),
     "ysb": ("sbuf", [128, 128 * N], "float32"),
     "chrow": ("sbuf", [128, 128], "float32"),
-    "chc": ("sbuf", [128, 64], "float32"),
-    "cht": ("sbuf", [128, 64], "float32"),
+    "chc": ("sbuf", [128, 32], "float32"),
+    "cht": ("sbuf", [128, 32], "float32"),
+    "chk": ("sbuf", [128, 24], "float32"),
+    "chm": ("sbuf", [128, 24], "float32"),
+    "chl": ("sbuf", [128, 8], "float32"),
     "chf": ("sbuf", [128, 8], "float32"),
     "chd": ("dram", [128, 1], "float32"),
     "chland": ("dram", [N, 128, 1], "float32"),
@@ -48,45 +61,39 @@ SCRATCH = {
     "psT": ("psum", [128, 512], "float32"),
     "psY": ("psum", [128, 1536], "float32"),
 }
+UNITS = ["own", "b0f", "b0s", "b1f", "w0", "w1"]
 SEMAPHORES = (
-    ["lq", "lx", "mo", "mf", "mk1", "mk2", "mtop", "mch", "qq", "qx", "qe", "ge", "gi", "gp"]
+    ["lq", "lx", "mo", "mf", "mk", "mtop", "mch", "ms", "qq", "qx", "qr", "qe", "ge", "gi", "gp", "gm"]
     + ["dm%d" % b for b in range(4)] + ["rs%d" % b for b in range(4)]
-    + ["sm%d%d" % (b, h) for b in range(2) for h in range(4)]
-    + ["sn%d%d" % (b, h) for b in range(2) for h in range(4)]
-    + ["tr%d%d" % (b, h) for b in range(2) for h in range(2)]
-    + [n + str(b) for n in ("rmx", "ltx", "ccx", "bcx", "ctx", "ofx") for b in range(2)]
-    + [n + str(j) for n in ("gv", "gs", "qz", "ym", "yc", "q", "d") for j in range(N)]
-    + ["yd", "chr", "chs", "chl", "chi", "chg", "cht1", "chf1", "cho", "sent", "hqc", "hqs"]
-    + [n + str(j) for n in ("hxc", "hxs") for j in range(2)]
+    + [n + u + str(h) for n in ("sm", "sn") for u in UNITS for h in range(2)]
+    + ["tr%d%d" % (b, h) for b in range(3) for h in range(2)]
+    + [n + str(b) for n in ("cel", "bcx", "ctx", "ofx", "pm", "pc", "yg") for b in range(3)]
+    + [n + str(j) for n in ("gv", "gs", "qz", "ym", "yc") for j in range(6)]
+    + [n + str(j) for n in ("q", "d") for j in range(N)]
+    + ["w" + str(i) + str(part) for i in range(2) for part in range(2)]
+    + ["yd", "ye", "chr", "chs", "chi", "chg", "chv", "chl1", "chf1", "cho", "sent"]
+    + ["hfc0", "hfs0", "hfc1", "hfs1", "hxc", "hxs"]
 )
-
-
-def classes(me, T, topo):
-    cores = T.cores
-    same = [r for r in range(N) if r == me or topo.same_plane(cores[me], cores[r])]
-    return same, [r for r in range(N) if r not in same]
-
-
-def slot(me, r, T, topo):
-    same, other = classes(me, T, topo)
-    return (same + other).index(r)
 
 
 def make_plan(me, T, topo):
     cores = T.cores
     core = cores[me]
-    same, other = classes(me, T, topo)
+    same = [r for r in range(N) if r == me or topo.same_plane(core, cores[r])]
+    other = [r for r in range(N) if r not in same]
     mate = [r for r in other if topo.mates(core, cores[r])][0]
     P = sorted([r for r in same if r != me], key=lambda r: r ^ me)
     X = sorted([r for r in other if r != mate], key=lambda r: r ^ me)
     relays = [c for c in topo.cores_of(core) if topo.die(c) != topo.die(core)
               and all(topo.may_write(c, cores[x]) for x in X)]
+    near2 = sorted([mate, X[2]])
     return {
-        "P": P, "M": mate, "X": X, "same": same, "other": other, "relays": relays,
-        "q_relay": {X[0]: 0, X[1]: 1},
-        "x_relay": {X[0]: (0, 0), P[2]: (1, 0), X[1]: (1, 1)},
-        "order": [P[0], P[2], P[1], X[0], X[1], X[2], mate, me],
-        "yorder": [P[0], P[2], P[1], me, X[0], X[2], X[1], mate],
+        "P": P, "M": mate, "X": X, "same": same, "relays": relays[:2], "W": sorted(X[:2]), "B": near2,
+        "slots": same + near2,
+        "w_relay": {X[0]: 0, X[1]: 1},
+        "x_relay": {P[0]: 0, P[2]: 1},
+        "first": [P[0], P[2], P[1]], "second": [X[2], mate],
+        "yorder": [P[0], P[1], P[2], X[2], mate],
     }
 
 
@@ -101,12 +108,14 @@ def rank_program(g, core, T, topo):
         if homes:
             relay_program(g, core, homes[0], T, topo)
         return
-    plan = make_plan(me, T, topo)
-    P, M, X, relays = plan["P"], plan["M"], plan["X"], plan["relays"]
+    plans = [make_plan(r, T, topo) for r in range(N)]
+    plan = plans[me]
+    P, M, X, W, B, relays = plan["P"], plan["M"], plan["X"], plan["W"], plan["B"], plan["relays"]
+    first, second = plan["first"], plan["second"]
+    chosen_ranks = first + second
     cores = T.cores
     sem = T.sem
-    order, yorder = plan["order"], plan["yorder"]
-    sl = {r: slot(me, r, T, topo) for r in range(N)}
+    sl = {r: j for j, r in enumerate(plan["slots"])}
     own = sl[me]
     u8 = dt.uint8
     Op = AluOpType
@@ -124,12 +133,16 @@ def rank_program(g, core, T, topo):
 
     V.memset(T.ob[:], 1.0).then_inc(sem.mo, 1)
     V.memset(T.onf[:], 1.0).then_inc(sem.mf, 1)
-    V.memset(T.msk[:], BIG).then_inc(sem.mk1, 1)
+    V.memset(T.msk[:], BIG).then_inc(sem.mk, 1)
     V.memset(T.top[:], BIG).then_inc(sem.mtop, 1)
+    V.memset(T.scol[:], 64.0).then_inc(sem.ms, 1)
     V.memset(T.chrow[:], 0.0).then_inc(sem.mch, 1)
     V.memset(T.chc[:], 0.0).then_inc(sem.mch, 1)
-    V.wait_ge(sem.mk1, 1)
-    V.memset(T.msk[:, 0:256:16], -BIG).then_inc(sem.mk2, 1)
+    V.memset(T.chl[:], 0.0).then_inc(sem.mch, 1)
+    V.wait_ge(sem.mk, 1)
+    V.memset(T.msk[:, 0:256:16], -BIG).then_inc(sem.mk, 1)
+    V.wait_ge(sem.ms, 1)
+    V.memset(T.scol[32 * own:32 * own + 32, :], 16.0).then_inc(sem.ms, 1)
     V.wait_ge(sem.lq, 16)
     V.quantize_mx(qcol(T.QC, own), qcol(T.QS, own), T.qwb[:]).then_inc(sem.qq, 1)
     V.wait_ge(sem.lx, 16)
@@ -141,6 +154,9 @@ def rank_program(g, core, T, topo):
         V.wait_ge(sem["dm%d" % b], 1)
         k = 512 * (b % 2)
         V.tensor_tensor(T.rb[:, b:1024:4], T.xb[:, b:1024:4], T.psD[:, k:k + 256], Op.subtract).then_inc(sem["rs%d" % b], 1)
+    for b in range(4):
+        V.wait_ge(sem["rs%d" % b], 1)
+    V.quantize_mx(T.RC[:], T.RS[:], T.rb[:]).then_inc(sem.qr, 1)
 
     PE.wait_ge(sem.qx, 1)
     PE.wait_ge(sem.qe, 4)
@@ -150,67 +166,69 @@ def rank_program(g, core, T, topo):
         k = 512 * (b % 2)
         PE.matmul_mx(T.psD[:, k:k + 256], qcol(T.EC, b), qcol(T.ES, b), T.XC[:], T.XS[:], True, True).then_inc(sem["dm%d" % b], 1)
 
-    def bank(pair, h):
-        return (T.psA, T.psY)[pair][:, 512 * h:512 * h + 256]
+    base, wide, step = (0, 1024, 1536), (512, 256, 256), (4, 2, 2)
+    fp = 1 - own // 2
+    single = own + 1 - 2 * (own % 2)
+    units = {"own": (0, 128 * own, 128, T.psY), "b0f": (0, 256 * fp, 256, T.psA), "b0s": (0, 128 * single, 128, T.psY),
+             "b1f": (1, 0, 256, T.psA), "w0": (2, 0, 128, T.psA), "w1": (2, 128, 128, T.psY)}
 
-    def scores_pe(bt):
-        ranks = (plan["same"], plan["other"])[bt]
-        for pair in range(2):
-            for r in ranks[2 * pair:2 * pair + 2]:
-                if r == me:
-                    PE.wait_ge(sem.qq, 1)
-                else:
-                    PE.wait_ge(sem["q%d" % r], 16)
-            k = 512 * bt + 256 * pair
-            for h in range(2):
-                PE.matmul_mx(bank(pair, h), qcol(T.XC, h), qcol(T.XS, h), T.QC[:, k:k + 256], T.QS[:, k:k + 256],
-                             True, True).then_inc(sem["sm%d%d" % (bt, 2 * pair + h)], 1)
-        if bt == 0:
-            PE.wait_ge(sem.gi, 1)
-        else:
-            PE.wait_ge(sem.ofx0, 4)
+    def score(u):
+        bt, a, n, ps = units[u]
         for h in range(2):
-            k = 1024 * bt + 512 * h
-            for pair in range(2):
-                PE.wait_ge(sem["sn%d%d" % (bt, 2 * pair + h)], 1)
-            PE.transpose(T.psT[:, 128 * h:128 * h + 128], T.sc[:, k + 3:k + 512:4], T.idn[:]).then_inc(sem["tr%d%d" % (bt, h)], 1)
+            if bt < 2:
+                k = 512 * bt + a
+                args = (qcol(T.XC, h), qcol(T.XS, h), T.QC[:, k:k + n], T.QS[:, k:k + n])
+            else:
+                k = 512 * (a // 128) + 128 * h
+                args = (T.FC[:, k:k + 128], T.FS[:, k:k + 128], qcol(T.QC, own), qcol(T.QS, own))
+            PE.matmul_mx(ps[:, 512 * h:512 * h + n], *args, True, True).then_inc(sem["sm%s%d" % (u, h)], 1)
+
+    def groups_v(u):
+        bt, a, n, ps = units[u]
+        for h in range(2):
+            k = base[bt] + wide[bt] * h + a
+            V.wait_ge(sem["sm%s%d" % (u, h)], 1)
+            V.tensor_tensor_scan(T.sc[:, k:k + n], T.msk[:, 0:n], ps[:, 512 * h:512 * h + n], -BIG, Op.min, Op.max).then_inc(sem["sn%s%d" % (u, h)], 1)
+
+    def turn(bt, us):
+        for h in range(2):
+            k = base[bt] + wide[bt] * h
+            for u in us:
+                PE.wait_ge(sem["sn%s%d" % (u, h)], 1)
+            PE.transpose(T.psT[:, 128 * h:128 * h + 128], T.sc[:, k + step[bt] - 1:k + wide[bt]:step[bt]], T.idn[:]).then_inc(sem["tr%d%d" % (bt, h)], 1)
+
+    def spread(bt):
         PE.wait_ge(sem["bcx%d" % bt], 1)
         PE.transpose(T.psT[:, 256:384], T.bc[:, 128 * bt:128 * bt + 128], T.idn[:]).then_inc(sem["ctx%d" % bt], 1)
 
-    def groups_v(bt):
-        if bt == 0:
-            V.wait_ge(sem.mk2, 1)
-        for pair in range(2):
-            for h in range(2):
-                k = 1024 * bt + 512 * h + 256 * pair
-                i = "%d%d" % (bt, 2 * pair + h)
-                V.wait_ge(sem["sm" + i], 1)
-                V.tensor_tensor_scan(T.sc[:, k:k + 256], T.msk[:], bank(pair, h), -BIG, Op.min, Op.max).then_inc(sem["sn" + i], 1)
-
     def cells_v(bt):
-        if bt == 0:
-            V.wait_ge(sem.mtop, 1)
         V.wait_ge(sem["tr%d0" % bt], 1)
         V.wait_ge(sem["tr%d1" % bt], 1)
-        rm = 256 * bt
-        V.tensor_tensor_scan(T.rm[:, rm:rm + 256], T.top[:], T.psT[:, 0:256], -BIG, Op.min, Op.max).then_inc(sem["rmx%d" % bt], 1)
-        V.wait_ge(sem["rmx%d" % bt], 1)
+        rm, done = 256 * bt, sem["cel%d" % bt]
+        V.tensor_tensor_scan(T.rm[:, rm:rm + 256], T.top[:], T.psT[:, 0:256], -BIG, Op.min, Op.max).then_inc(done, 1)
+        V.wait_ge(done, 1)
         lt = T.ltb[:, 16 * bt:16 * bt + 16]
-        V.tensor_scalar(lt, T.rm[:, rm + 15:rm + 256:16], T.rm[:, rm + 255:rm + 256], 64.0, Op.is_lt, Op.mult).then_inc(sem["ltx%d" % bt], 1)
-        V.wait_ge(sem["ltx%d" % bt], 1)
-        V.tensor_reduce(T.cc[:, 4 * bt:4 * bt + 1], lt, AxisListType.X, Op.add).then_inc(sem["ccx%d" % bt], 1)
-        V.wait_ge(sem["ccx%d" % bt], 1)
-        if bt == 0:
-            V.wait_ge(sem.gp, 1)
+        unit = (T.scol[:, 0:1], 64.0, 16.0)[bt]
+        V.tensor_scalar(lt, T.rm[:, rm + 15:rm + 256:16], T.rm[:, rm + 255:rm + 256], unit, Op.is_lt, Op.mult).then_inc(done, 1)
+        V.wait_ge(done, 2)
+        V.tensor_reduce(T.cc[:, 4 * bt:4 * bt + 1], lt, AxisListType.X, Op.add).then_inc(done, 1)
+        V.wait_ge(done, 3)
         V.tensor_scalar(T.bc[:, 128 * bt:128 * bt + 128], T.p16[:], T.cc[:, 4 * bt:4 * bt + 1], None, Op.add).then_inc(sem["bcx%d" % bt], 1)
 
     def lists_v(bt):
         V.wait_ge(sem["ctx%d" % bt], 1)
+        s = 2 * step[bt] * 2 if bt else 4
+        src = T.psT[:, 256 + s - 1:384:s]
+        if bt == 2:
+            V.tensor_scalar(T.offl[:, 8:24], src, 0.0, None, Op.add).then_inc(sem.ofx2, 1)
+            V.wait_ge(sem.ofx2, 2)
+            return
+        end = (128, 192)[bt]
         for e in range(4):
-            V.tensor_scalar(T.off[:, 128 * bt + e:128 * bt + 128:4], T.psT[:, 259:384:4], 16.0 * e, None, Op.add).then_inc(sem["ofx%d" % bt], 1)
+            V.tensor_scalar(T.off[:, 128 * bt + e:end:4], src, 16.0 * e, None, Op.add).then_inc(sem["ofx%d" % bt], 1)
         V.wait_ge(sem["ofx%d" % bt], 4)
 
-    share = {r: (14 if r in order[:3] else 28) for r in range(N)}
+    share = {r: (22 if r in first else 18) for r in chosen_ranks}
 
     def gather_s(r):
         j, k = sl[r], share[r]
@@ -227,16 +245,66 @@ def rank_program(g, core, T, topo):
         V.wait_ge(sem["gs%d" % j], 2)
         V.quantize_mx(xcol(T.OC, j), xcol(T.OS, j), T.hb[:, 1024 * j:1024 * j + 1024]).then_inc(sem["qz%d" % j], 1)
 
-    first, second = order[:3], order[3:]
+    whole = [me] + W
 
-    scores_pe(0)
-    scores_pe(1)
+    def pick_v(i):
+        s = whole[i]
+        V.wait_ge(sem["pc%d" % i], 1)
+        V.tensor_copy(T.ysb[:, 128 * s:128 * s + 128], T.pf[:, 256 * i:256 * i + 256].indirect(T.offl[:, 8 * i:8 * i + 8])).then_inc(sem["yg%d" % i], 1)
 
-    groups_v(0)
+    def full(i, ps, parts):
+        for part, (c, p) in enumerate(parts):
+            mm = PE.matmul_mx(ps, qcol(T.QC, own), qcol(T.QS, own), c, p, part == 0, part == 1)
+        mm.then_inc(sem["pm%d" % i], 1)
+
+    def wparts(f):
+        return [(xcol(T.FC, 2 * f + part), xcol(T.FS, 2 * f + part)) for part in range(2)]
+
+    bankA = [T.psA[:, 0:256], T.psA[:, 512:768]]
+    bankY = [T.psY[:, 512 * i:512 * i + 256] for i in range(3)]
+    PE.wait_ge(sem.qq, 1)
+    score("own")
+    for j in (2 * fp, 2 * fp + 1):
+        PE.wait_ge(sem["q%d" % plan["slots"][j]], 16)
+    score("b0f")
+    PE.wait_ge(sem["q%d" % plan["slots"][single]], 16)
+    PE.wait_ge(sem.snown0, 1)
+    PE.wait_ge(sem.snown1, 1)
+    score("b0s")
+    PE.wait_ge(sem.qr, 1)
+    full(0, bankY[2], [(T.XC[:], T.XS[:]), (T.RC[:], T.RS[:])])
+    PE.wait_ge(sem.gi, 1)
+    turn(0, ["own", "b0f", "b0s"])
+    spread(0)
+    for r in B:
+        PE.wait_ge(sem["q%d" % r], 16)
+    score("b1f")
+    PE.wait_ge(sem.ofx0, 4)
+    turn(1, ["b1f"])
+    spread(1)
+    for f in range(2):
+        PE.wait_ge(sem["w%d0" % f], 16)
+        score("w%d" % f)
+    PE.wait_ge(sem.pc0, 1)
+    PE.wait_ge(sem.w01, 16)
+    full(1, bankY[2], wparts(0))
+    PE.wait_ge(sem.ofx1, 4)
+    turn(2, ["w0", "w1"])
+    PE.wait_ge(sem.w11, 16)
+    full(2, bankA[0], wparts(1))
+    spread(2)
+
+    V.wait_ge(sem.mk, 2)
+    V.wait_ge(sem.mtop, 1)
+    groups_v("own")
+    groups_v("b0f")
+    groups_v("b0s")
+    V.wait_ge(sem.gp, 2)
+    V.wait_ge(sem.ms, 2)
     cells_v(0)
     lists_v(0)
     gather_v(first[0])
-    groups_v(1)
+    groups_v("b1f")
     pack_v(first[0])
     gather_v(first[1])
     cells_v(1)
@@ -245,21 +313,36 @@ def rank_program(g, core, T, topo):
     lists_v(1)
     gather_v(second[0])
     pack_v(first[2])
-    V.wait_ge(sem.mch, 2)
-    V.tensor_scalar(T.chrow[0:1, 0:64], T.off[0:1, 0:256:4], 1.0 / 64.0, None, Op.mult).then_inc(sem.chr, 1)
+    gather_v(second[1])
+    V.wait_ge(sem.mch, 3)
+    V.tensor_scalar(T.chrow[0:1, 0:48], T.off[0:1, 0:192:4], 1.0 / 64.0, None, Op.mult).then_inc(sem.chr, 1)
     pack_v(second[0])
-    for r in second[1:]:
-        gather_v(r)
-        pack_v(r)
+    groups_v("w0")
+    groups_v("w1")
+    pack_v(second[1])
+    V.tensor_scalar(T.offl[:, 0:8], T.off[:, 32 * own:32 * own + 32:4], 0.0, None, Op.add).then_inc(sem.ofx2, 1)
+    V.wait_ge(sem.ofx2, 1)
+    pick_v(0)
+    cells_v(2)
+    lists_v(2)
+    pick_v(1)
+    pick_v(2)
+
+    def keep_s(i, ps):
+        S.wait_ge(sem["pm%d" % i], 1)
+        S.activation(T.pf[:, 256 * i:256 * i + 256], ps, Copy).then_inc(sem["pc%d" % i], 1)
 
     for b in range(4):
         S.wait_ge(sem["rs%d" % b], 1)
+    keep_s(0, bankY[2])
     S.wait_ge(sem.ofx0, 4)
     for r in first:
         gather_s(r)
     S.wait_ge(sem.ofx1, 4)
     for r in second:
         gather_s(r)
+    keep_s(1, bankY[2])
+    keep_s(2, bankA[0])
 
     sent = [0]
 
@@ -279,106 +362,100 @@ def rank_program(g, core, T, topo):
         far &= topo.mask(core, cores[r])
     near = topo.mask(core, relays[0]) & topo.mask(core, relays[1]) & ~far
 
+    g.iota(T.p16[:], [[0, 8], [1, 16]], 0, 0, allow_small_or_imprecise_dtypes=True).then_inc(sem.gp, 1)
+    g.iota(T.pcol[:], [[0, 8]], 0, 1, allow_small_or_imprecise_dtypes=True).then_inc(sem.gp, 1)
     g.wait_ge(sem.mo, 1)
     g.affine_select(T.eb[:], T.ob[:], [[-1, 528]], Op.is_equal, 0.0, 4, 4).then_inc(sem.ge, 1)
 
     g.wait_ge(sem.qq, 1)
-    straight = [M] + [x for x in X if x not in plan["q_relay"]]
-    helpers = [relays[i] for i in sorted(plan["q_relay"].values())]
-
-    def qpair(buf, ranks):
-        out = []
-        for r in ranks:
-            v = qcol(T[buf], slot(r, me, T, topo))
-            out.append((cores[r], v.bitcast(u8) if buf == "QC" else v))
-        return out
-
     qsem = sem["q%d" % me]
-    post(tr(qcol(T.QC, own).bitcast(u8), qpair("QC", P), far, qsem),
-         tr(qcol(T.QC, own).bitcast(u8), [(c, T.HQC[:].bitcast(u8)) for c in helpers], near, sem.hqc))
-    post(tr(qcol(T.QS, own), qpair("QS", P), far, qsem),
-         tr(qcol(T.QS, own), [(c, T.HQS[:]) for c in helpers], near, sem.hqs))
-    post(tr(qcol(T.QC, own).bitcast(u8), qpair("QC", straight), far, qsem))
-    post(tr(qcol(T.QS, own), qpair("QS", straight), far, qsem))
+    for ranks in (P, B):
+        at = [(cores[r], plans[r]["slots"].index(me)) for r in ranks]
+        post(tr(qcol(T.QC, own).bitcast(u8), [(c, qcol(T.QC, j).bitcast(u8)) for c, j in at], far, qsem))
+        post(tr(qcol(T.QS, own), [(c, qcol(T.QS, j)) for c, j in at], far, qsem))
 
     g.wait_ge(sem.mf, 1)
     g.affine_select(T.idn[:], T.onf[:], [[-1, 128]], Op.is_equal, 0.0, 0, 1).then_inc(sem.gi, 1)
-    g.iota(T.p16[:], [[0, 8], [1, 16]], 0, 0, allow_small_or_imprecise_dtypes=True).then_inc(sem.gp, 1)
 
-    dsem = sem["d%d" % me]
+    for part, (c, p, ready) in enumerate(((T.XC, T.XS, sem.qx), (T.RC, T.RS, sem.qr))):
+        g.wait_ge(ready, 1)
+        post(tr(c[:].bitcast(u8), [(h, xcol(T.HFC, part).bitcast(u8)) for h in relays], near, sem["hfc%d" % part]))
+        post(tr(p[:], [(h, xcol(T.HFS, part)) for h in relays], near, sem["hfs%d" % part]))
+    g.affine_select(T.m24[:], T.onf[:, 0:24], [[0, 3], [-1, 8]], Op.is_equal, 0.0, 0, 1).then_inc(sem.gm, 1)
 
-    def chosen(ranks):
-        for r in ranks:
-            g.wait_ge(sem["qz%d" % sl[r]], 1)
-        codes, planes = [], []
-        for r in ranks:
-            j, k = sl[r], slot(r, me, T, topo)
-            if r in plan["x_relay"]:
-                i, n = plan["x_relay"][r]
-                codes.append(tr(xcol(T.OC, j).bitcast(u8), [(relays[i], xcol(T.HXC, n).bitcast(u8))], near, sem["hxc%d" % n]))
-                planes.append(tr(xcol(T.OS, j), [(relays[i], xcol(T.HXS, n))], near, sem["hxs%d" % n]))
-            else:
-                codes.append(tr(xcol(T.OC, j).bitcast(u8), [(cores[r], xcol(T.LC, k).bitcast(u8))], far, dsem))
-                planes.append(tr(xcol(T.OS, j), [(cores[r], xcol(T.LS, k))], far, dsem))
-        post(*codes)
-        post(*planes)
+    def send_chosen(r):
+        j = sl[r]
+        g.wait_ge(sem["qz%d" % j], 1)
+        if r in plan["x_relay"]:
+            h = relays[plan["x_relay"][r]]
+            post(tr(xcol(T.OC, j).bitcast(u8), [(h, T.HXC[:].bitcast(u8))], near, sem.hxc))
+            post(tr(xcol(T.OS, j), [(h, T.HXS[:])], near, sem.hxs))
+        else:
+            k = plans[r]["slots"].index(me)
+            post(tr(xcol(T.OC, j).bitcast(u8), [(cores[r], xcol(T.LC, k).bitcast(u8))], far, sem["d%d" % me]))
+            post(tr(xcol(T.OS, j), [(cores[r], xcol(T.LS, k))], far, sem["d%d" % me]))
 
-    chosen([P[0], P[2]])
-    chosen([P[1]])
-    chosen([X[0]])
-    chosen([X[1]])
-    chosen([X[2]])
+    for r in chosen_ranks[:-1]:
+        send_chosen(r)
     one = 1 << topo.engines(core, cores[M])[0]
     g.wait_ge(sem.chs, 16)
-    post(tr(T.chd[:], [(cores[r], T.chland[slot(r, me, T, topo)]) for r in P + [M] + X], one, sem.chi))
-    chosen([M])
+    post(tr(T.chd[:], [(cores[r], T.chland[me]) for r in chosen_ranks], one, sem.chi))
+    send_chosen(chosen_ranks[-1])
     g.wait_ge(sem.sent, sent[0])
 
-    for i, s in enumerate(yorder):
-        j, k = sl[s], 512 * (i % 3)
-        if s == me:
-            PE.wait_ge(sem["qz%d" % j], 1)
-            cod, sca = T.OC, T.OS
-        else:
-            PE.wait_ge(sem["d%d" % s], 16)
-            cod, sca = T.LC, T.LS
+    ybank = [T.psY[:, 0:128], T.psY[:, 512:640], T.psA[:, 512:640], T.psY[:, 1024:1152], T.psA[:, 0:128]]
+    for i, s in enumerate(plan["yorder"]):
+        j = sl[s]
+        PE.wait_ge(sem["d%d" % s], 16)
         if i >= 3:
-            PE.wait_ge(sem["yc%d" % sl[yorder[i - 3]]], 1)
+            PE.wait_ge(sem["pc%d" % (i - 2)], 1)
         for part in range(2):
             a = 256 * j + 128 * part
-            mm = PE.matmul_mx(T.psY[:, k:k + 128], qcol(T.QC, own), qcol(T.QS, own),
-                              cod[:, a:a + 128], sca[:, a:a + 128], part == 0, part == 1)
+            mm = PE.matmul_mx(ybank[i], qcol(T.QC, own), qcol(T.QS, own), T.LC[:, a:a + 128], T.LS[:, a:a + 128], part == 0, part == 1)
         mm.then_inc(sem["ym%d" % j], 1)
         S.wait_ge(sem["ym%d" % j], 1)
-        S.activation(T.ysb[:, 128 * s:128 * s + 128], T.psY[:, k:k + 128], Copy).then_inc(sem["yc%d" % j], 1)
+        S.activation(T.ysb[:, 128 * s:128 * s + 128], ybank[i], Copy).then_inc(sem["yc%d" % j], 1)
         S.wait_ge(sem["yc%d" % j], 1)
         S.dma_start(T.y[:, 128 * s:128 * s + 128], T.ysb[:, 128 * s:128 * s + 128]).then_inc(sem.yd, 16)
-    S.wait_ge(sem.yd, 16 * N)
+    S.wait_ge(sem.yd, 16 * len(plan["yorder"]))
 
     SY.wait_ge(sem.chr, 1)
     SY.dma_start(T.chd[:], T.chrow[0:1, :]).then_inc(sem.chs, 16)
-    SY.dma_start(T.chland[own], T.chrow[0:1, :]).then_inc(sem.chl, 16)
-    SY.wait_ge(sem.chl, 16)
-    SY.wait_ge(sem.chi, N - 1)
-    SY.wait_ge(sem.mch, 2)
-    i = plan["same"].index(me)
-    half = len(plan["same"])
-    SY.dma_start(T.chc[0:half, 0:8], T.chland[0:half, 8 * i:8 * i + 8, 0]).then_inc(sem.chg, 16)
-    c0 = 8 * half + 8 * i
-    SY.dma_start(T.chc[0:N - half, 32:40], T.chland[half:N, c0:c0 + 8, 0]).then_inc(sem.chg, 16)
-    V.wait_ge(sem.chg, 32)
-    V.transpose(T.cht[0:32, :], T.chc[0:32, :]).then_inc(sem.cht1, 1)
-    V.wait_ge(sem.cht1, 1)
-    for n, cl in enumerate((plan["same"], plan["other"])):
-        V.tensor_copy(T.chf[0:8, cl[0]:cl[-1] + 1:cl[1] - cl[0]], T.cht[0:8, 32 * n:32 * n + len(cl)]).then_inc(sem.chf1, 1)
-    SY.wait_ge(sem.chf1, 2)
+
+    def store_sy(i):
+        s = whole[i]
+        SY.wait_ge(sem["yg%d" % i], 1)
+        SY.dma_start(T.y[:, 128 * s:128 * s + 128], T.ysb[:, 128 * s:128 * s + 128]).then_inc(sem.ye, 16)
+
+    store_sy(0)
+    SY.wait_ge(sem.chi, len(chosen_ranks))
+    SY.wait_ge(sem.mch, 3)
+    for s in chosen_ranks:
+        a = 8 * plans[s]["slots"].index(me)
+        SY.dma_start(T.chc[s:s + 1, 0:8], T.chland[s:s + 1, a:a + 8, 0]).then_inc(sem.chg, 16)
+    store_sy(1)
+    store_sy(2)
+    V.tensor_scalar(T.chk[0:8, :], T.offl[0:8, 0:24], T.pcol[0:8, 0:1], 1.0 / 16.0, Op.subtract, Op.mult).then_inc(sem.chv, 1)
+    V.wait_ge(sem.chv, 1)
+    V.wait_ge(sem.gm, 1)
+    V.tensor_tensor(T.chm[0:8, :], T.chk[0:8, :], T.m24[0:8, :], Op.mult).then_inc(sem.chv, 1)
+    V.wait_ge(sem.chv, 2)
+    for i, s in enumerate(whole):
+        V.tensor_reduce(T.chl[0:8, s:s + 1], T.chm[0:8, 8 * i:8 * i + 8], AxisListType.X, Op.add).then_inc(sem.chl1, 1)
+    V.wait_ge(sem.chg, 16 * len(chosen_ranks))
+    V.transpose(T.cht[0:32, :], T.chc[0:32, :]).then_inc(sem.chv, 1)
+    V.wait_ge(sem.chv, 3)
+    V.wait_ge(sem.chl1, len(whole))
+    V.tensor_tensor(T.chf[0:8, :], T.cht[0:8, 0:8], T.chl[0:8, :], Op.add).then_inc(sem.chf1, 1)
+    SY.wait_ge(sem.chf1, 1)
     SY.dma_start(T.ch[:], T.chf[0:8, :]).then_inc(sem.cho, 16)
     SY.wait_ge(sem.cho, 16)
+    SY.wait_ge(sem.ye, 16 * len(whole))
 
 
 def relay_program(g, core, me, T, topo):
     plan = make_plan(me, T, topo)
-    if core not in plan["relays"][:2]:
+    if core not in plan["relays"]:
         return
     cores, sem = T.cores, T.sem
     which = plan["relays"].index(core)
@@ -388,25 +465,26 @@ def relay_program(g, core, me, T, topo):
     u8 = dt.uint8
     sent = [0]
 
-    def send(dst, out, src, rsem):
+    def send(wait, dst, out, src, rsem):
+        g.wait_ge(wait, arrive)
         rid, pid = topo.addr(dst, core)
         mask = topo.mask(core, dst)
         sent[0] += count(mask)
         g.remote_dma_fused([RemoteDMATransfer(dst_ids=[DstId(rid=rid, pnc=pid)], dma_engine_mask=mask, remote_sem=rsem,
                                               srcs=[src], dsts=[out])], local_sem=sem.sent)
 
-    for r, i in plan["q_relay"].items():
+    for r, i in plan["w_relay"].items():
         if i == which:
-            k = 128 * slot(r, me, T, topo)
-            g.wait_ge(sem.hqc, arrive)
-            send(cores[r], T.QC[:, k:k + 128].bitcast(u8), T.HQC[:].bitcast(u8), sem["q%d" % me])
-            g.wait_ge(sem.hqs, arrive)
-            send(cores[r], T.QS[:, k:k + 128], T.HQS[:], sem["q%d" % me])
-    jobs = sorted((n, r) for r, (i, n) in plan["x_relay"].items() if i == which)
-    for n, r in jobs:
-        k = 256 * slot(r, me, T, topo)
-        g.wait_ge(sem["hxc%d" % n], arrive)
-        send(cores[r], T.LC[:, k:k + 256].bitcast(u8), T.HXC[:, 256 * n:256 * n + 256].bitcast(u8), sem["d%d" % me])
-        g.wait_ge(sem["hxs%d" % n], arrive)
-        send(cores[r], T.LS[:, k:k + 256], T.HXS[:, 256 * n:256 * n + 256], sem["d%d" % me])
+            f = make_plan(r, T, topo)["W"].index(me)
+            for part in range(2):
+                a, k = 256 * part, 512 * f + 256 * part
+                there = sem["w%d%d" % (f, part)]
+                send(sem["hfc%d" % part], cores[r], T.FC[:, k:k + 256].bitcast(u8), T.HFC[:, a:a + 256].bitcast(u8), there)
+                send(sem["hfs%d" % part], cores[r], T.FS[:, k:k + 256], T.HFS[:, a:a + 256], there)
+    for r, i in plan["x_relay"].items():
+        if i == which:
+            k = 256 * make_plan(r, T, topo)["slots"].index(me)
+            there = sem["d%d" % me]
+            send(sem.hxc, cores[r], T.LC[:, k:k + 256].bitcast(u8), T.HXC[:].bitcast(u8), there)
+            send(sem.hxs, cores[r], T.LS[:, k:k + 256], T.HXS[:], there)
     g.wait_ge(sem.sent, sent[0])

from concourse.bass import DstId, RemoteDMATransfer
from concourse.mybir import dt, AluOpType, AxisListType, ActivationFunctionType

N = 8
BIG = 1e29
CODES, PLANE = "float8_e4m3fn_x4", "uint8"

SCRATCH = {
    "qwb": ("sbuf", [128, 512], "bfloat16"),
    "xb": ("sbuf", [128, 1024], "bfloat16"),
    "rb": ("sbuf", [128, 1024], "bfloat16"),
    "ob": ("sbuf", [128, 528], "bfloat16"),
    "eb": ("sbuf", [128, 528], "bfloat16"),
    "onf": ("sbuf", [128, 128], "float32"),
    "idn": ("sbuf", [128, 128], "float32"),
    "p16": ("sbuf", [128, 128], "float32"),
    "pcol": ("sbuf", [128, 8], "float32"),
    "m24": ("sbuf", [128, 24], "float32"),
    "scol": ("sbuf", [128, 8], "float32"),
    "msk": ("sbuf", [128, 256], "float32"),
    "top": ("sbuf", [128, 256], "float32"),
    "QC": ("sbuf", [128, 128 * 6], CODES),
    "QS": ("sbuf", [128, 128 * 6], PLANE),
    "XC": ("sbuf", [128, 256], CODES),
    "XS": ("sbuf", [128, 256], PLANE),
    "RC": ("sbuf", [128, 256], CODES),
    "RS": ("sbuf", [128, 256], PLANE),
    "EC": ("sbuf", [128, 512], CODES),
    "ES": ("sbuf", [128, 512], PLANE),
    "sc": ("sbuf", [128, 2048], "float32"),
    "rm": ("sbuf", [128, 768], "float32"),
    "ltb": ("sbuf", [128, 48], "float32"),
    "cc": ("sbuf", [128, 12], "float32"),
    "bc": ("sbuf", [128, 384], "float32"),
    "off": ("sbuf", [128, 32 * 6], "uint16"),
    "offl": ("sbuf", [128, 32], "uint16"),
    "hb": ("sbuf", [128, 1024 * 6], "bfloat16"),
    "OC": ("sbuf", [128, 256 * 6], CODES),
    "OS": ("sbuf", [128, 256 * 6], PLANE),
    "LC": ("sbuf", [128, 256 * 6], CODES),
    "LS": ("sbuf", [128, 256 * 6], PLANE),
    "FC": ("sbuf", [128, 1024], CODES),
    "FS": ("sbuf", [128, 1024], PLANE),
    "HFC": ("sbuf", [128, 512], CODES),
    "HFS": ("sbuf", [128, 512], PLANE),
    "HXC": ("sbuf", [128, 256], CODES),
    "HXS": ("sbuf", [128, 256], PLANE),
    "pf": ("sbuf", [128, 768], "float32"),
    "ysb": ("sbuf", [128, 128 * N], "float32"),
    "chrow": ("sbuf", [128, 128], "float32"),
    "chc": ("sbuf", [128, 32], "float32"),
    "cht": ("sbuf", [128, 32], "float32"),
    "chk": ("sbuf", [128, 24], "float32"),
    "chm": ("sbuf", [128, 24], "float32"),
    "chl": ("sbuf", [128, 8], "float32"),
    "chf": ("sbuf", [128, 8], "float32"),
    "chd": ("dram", [128, 1], "float32"),
    "chland": ("dram", [N, 128, 1], "float32"),
    "psD": ("psum", [128, 1024], "float32"),
    "psA": ("psum", [128, 1024], "float32"),
    "psT": ("psum", [128, 512], "float32"),
    "psY": ("psum", [128, 1536], "float32"),
}
UNITS = ["own", "b0f", "b0s", "b1f", "w0", "w1"]
SEMAPHORES = (
    ["lq", "lx", "mo", "mf", "mk", "mtop", "mch", "ms", "qq", "qx", "qr", "qe", "ge", "gi", "gp", "gm"]
    + ["dm%d" % b for b in range(4)] + ["rs%d" % b for b in range(4)]
    + [n + u + str(h) for n in ("sm", "sn") for u in UNITS for h in range(2)]
    + ["tr%d%d" % (b, h) for b in range(3) for h in range(2)]
    + [n + str(b) for n in ("cel", "bcx", "ctx", "ofx", "pm", "pc", "yg") for b in range(3)]
    + [n + str(j) for n in ("gv", "gs", "qz", "ym", "yc") for j in range(6)]
    + [n + str(j) for n in ("q", "d") for j in range(N)]
    + ["w" + str(i) + str(part) for i in range(2) for part in range(2)]
    + ["yd", "ye", "chr", "chs", "chi", "chg", "chv", "chl1", "chf1", "cho", "sent"]
    + ["hfc0", "hfs0", "hfc1", "hfs1", "hxc", "hxs"]
)


def make_plan(me, T, topo):
    cores = T.cores
    core = cores[me]
    same = [r for r in range(N) if r == me or topo.same_plane(core, cores[r])]
    other = [r for r in range(N) if r not in same]
    mate = [r for r in other if topo.mates(core, cores[r])][0]
    P = sorted([r for r in same if r != me], key=lambda r: r ^ me)
    X = sorted([r for r in other if r != mate], key=lambda r: r ^ me)
    relays = [c for c in topo.cores_of(core) if topo.die(c) != topo.die(core)
              and all(topo.may_write(c, cores[x]) for x in X)]
    near2 = sorted([mate, X[2]])
    return {
        "P": P, "M": mate, "X": X, "same": same, "relays": relays[:2], "W": sorted(X[:2]), "B": near2,
        "slots": same + near2,
        "w_relay": {X[0]: 0, X[1]: 1},
        "x_relay": {P[0]: 0, P[2]: 1},
        "first": [P[0], P[2], P[1]], "second": [X[2], mate],
        "yorder": [P[0], P[1], P[2], X[2], mate],
    }


def count(mask):
    return bin(mask).count("1")


def rank_program(g, core, T, topo):
    me = T.rank_of(core)
    if me is None:
        homes = [T.rank_of(c) for c in topo.cores_of(core) if T.rank_of(c) is not None]
        if homes:
            relay_program(g, core, homes[0], T, topo)
        return
    plans = [make_plan(r, T, topo) for r in range(N)]
    plan = plans[me]
    P, M, X, W, B, relays = plan["P"], plan["M"], plan["X"], plan["W"], plan["B"], plan["relays"]
    first, second = plan["first"], plan["second"]
    chosen_ranks = first + second
    cores = T.cores
    sem = T.sem
    sl = {r: j for j, r in enumerate(plan["slots"])}
    own = sl[me]
    u8 = dt.uint8
    Op = AluOpType
    Copy = ActivationFunctionType.Copy
    V, S, PE, SY = g.vector, g.scalar, g.tensor, g.sync

    def qcol(t, j):
        return t[:, 128 * j:128 * j + 128]

    def xcol(t, j):
        return t[:, 256 * j:256 * j + 256]

    SY.dma_start(T.qwb[:], T.qw[:]).then_inc(sem.lq, 16)
    S.dma_start(T.xb[:], T.x[:]).then_inc(sem.lx, 16)

    V.memset(T.ob[:], 1.0).then_inc(sem.mo, 1)
    V.memset(T.onf[:], 1.0).then_inc(sem.mf, 1)
    V.memset(T.msk[:], BIG).then_inc(sem.mk, 1)
    V.memset(T.top[:], BIG).then_inc(sem.mtop, 1)
    V.memset(T.scol[:], 64.0).then_inc(sem.ms, 1)
    V.memset(T.chrow[:], 0.0).then_inc(sem.mch, 1)
    V.memset(T.chc[:], 0.0).then_inc(sem.mch, 1)
    V.memset(T.chl[:], 0.0).then_inc(sem.mch, 1)
    V.wait_ge(sem.mk, 1)
    V.memset(T.msk[:, 0:256:16], -BIG).then_inc(sem.mk, 1)
    V.wait_ge(sem.ms, 1)
    V.memset(T.scol[32 * own:32 * own + 32, :], 16.0).then_inc(sem.ms, 1)
    V.wait_ge(sem.lq, 16)
    V.quantize_mx(qcol(T.QC, own), qcol(T.QS, own), T.qwb[:]).then_inc(sem.qq, 1)
    V.wait_ge(sem.lx, 16)
    V.quantize_mx(T.XC[:], T.XS[:], T.xb[:]).then_inc(sem.qx, 1)
    V.wait_ge(sem.ge, 1)
    for b in range(4):
        V.quantize_mx(qcol(T.EC, b), qcol(T.ES, b), T.eb[:, 4 - b:516 - b]).then_inc(sem.qe, 1)
    for b in range(4):
        V.wait_ge(sem["dm%d" % b], 1)
        k = 512 * (b % 2)
        V.tensor_tensor(T.rb[:, b:1024:4], T.xb[:, b:1024:4], T.psD[:, k:k + 256], Op.subtract).then_inc(sem["rs%d" % b], 1)
    for b in range(4):
        V.wait_ge(sem["rs%d" % b], 1)
    V.quantize_mx(T.RC[:], T.RS[:], T.rb[:]).then_inc(sem.qr, 1)

    PE.wait_ge(sem.qx, 1)
    PE.wait_ge(sem.qe, 4)
    for b in range(4):
        if b >= 2:
            PE.wait_ge(sem["rs%d" % (b - 2)], 1)
        k = 512 * (b % 2)
        PE.matmul_mx(T.psD[:, k:k + 256], qcol(T.EC, b), qcol(T.ES, b), T.XC[:], T.XS[:], True, True).then_inc(sem["dm%d" % b], 1)

    base, wide, step = (0, 1024, 1536), (512, 256, 256), (4, 2, 2)
    fp = 1 - own // 2
    single = own + 1 - 2 * (own % 2)
    units = {"own": (0, 128 * own, 128, T.psY), "b0f": (0, 256 * fp, 256, T.psA), "b0s": (0, 128 * single, 128, T.psY),
             "b1f": (1, 0, 256, T.psA), "w0": (2, 0, 128, T.psA), "w1": (2, 128, 128, T.psY)}

    def score(u):
        bt, a, n, ps = units[u]
        for h in range(2):
            if bt < 2:
                k = 512 * bt + a
                args = (qcol(T.XC, h), qcol(T.XS, h), T.QC[:, k:k + n], T.QS[:, k:k + n])
            else:
                k = 512 * (a // 128) + 128 * h
                args = (T.FC[:, k:k + 128], T.FS[:, k:k + 128], qcol(T.QC, own), qcol(T.QS, own))
            PE.matmul_mx(ps[:, 512 * h:512 * h + n], *args, True, True).then_inc(sem["sm%s%d" % (u, h)], 1)

    def groups_v(u):
        bt, a, n, ps = units[u]
        for h in range(2):
            k = base[bt] + wide[bt] * h + a
            V.wait_ge(sem["sm%s%d" % (u, h)], 1)
            V.tensor_tensor_scan(T.sc[:, k:k + n], T.msk[:, 0:n], ps[:, 512 * h:512 * h + n], -BIG, Op.min, Op.max).then_inc(sem["sn%s%d" % (u, h)], 1)

    def turn(bt, us):
        for h in range(2):
            k = base[bt] + wide[bt] * h
            for u in us:
                PE.wait_ge(sem["sn%s%d" % (u, h)], 1)
            PE.transpose(T.psT[:, 128 * h:128 * h + 128], T.sc[:, k + step[bt] - 1:k + wide[bt]:step[bt]], T.idn[:]).then_inc(sem["tr%d%d" % (bt, h)], 1)

    def spread(bt):
        PE.wait_ge(sem["bcx%d" % bt], 1)
        PE.transpose(T.psT[:, 256:384], T.bc[:, 128 * bt:128 * bt + 128], T.idn[:]).then_inc(sem["ctx%d" % bt], 1)

    def cells_v(bt):
        V.wait_ge(sem["tr%d0" % bt], 1)
        V.wait_ge(sem["tr%d1" % bt], 1)
        rm, done = 256 * bt, sem["cel%d" % bt]
        V.tensor_tensor_scan(T.rm[:, rm:rm + 256], T.top[:], T.psT[:, 0:256], -BIG, Op.min, Op.max).then_inc(done, 1)
        V.wait_ge(done, 1)
        lt = T.ltb[:, 16 * bt:16 * bt + 16]
        unit = (T.scol[:, 0:1], 64.0, 16.0)[bt]
        V.tensor_scalar(lt, T.rm[:, rm + 15:rm + 256:16], T.rm[:, rm + 255:rm + 256], unit, Op.is_lt, Op.mult).then_inc(done, 1)
        V.wait_ge(done, 2)
        V.tensor_reduce(T.cc[:, 4 * bt:4 * bt + 1], lt, AxisListType.X, Op.add).then_inc(done, 1)
        V.wait_ge(done, 3)
        V.tensor_scalar(T.bc[:, 128 * bt:128 * bt + 128], T.p16[:], T.cc[:, 4 * bt:4 * bt + 1], None, Op.add).then_inc(sem["bcx%d" % bt], 1)

    def lists_v(bt):
        V.wait_ge(sem["ctx%d" % bt], 1)
        s = 2 * step[bt] * 2 if bt else 4
        src = T.psT[:, 256 + s - 1:384:s]
        if bt == 2:
            V.tensor_scalar(T.offl[:, 8:24], src, 0.0, None, Op.add).then_inc(sem.ofx2, 1)
            V.wait_ge(sem.ofx2, 2)
            return
        end = (128, 192)[bt]
        for e in range(4):
            V.tensor_scalar(T.off[:, 128 * bt + e:end:4], src, 16.0 * e, None, Op.add).then_inc(sem["ofx%d" % bt], 1)
        V.wait_ge(sem["ofx%d" % bt], 4)

    share = {r: (22 if r in first else 18) for r in chosen_ranks}

    def gather_s(r):
        j, k = sl[r], share[r]
        S.activation(T.hb[:, 1024 * j + 16 * k:1024 * j + 512], T.xb[:, 0:1024].indirect(T.off[:, 32 * j + k:32 * j + 32]), Copy).then_inc(sem["gs%d" % j], 1)
        S.activation(T.hb[:, 1024 * j + 512:1024 * j + 1024], T.rb[:, 0:1024].indirect(T.off[:, 32 * j:32 * j + 32]), Copy).then_inc(sem["gs%d" % j], 1)

    def gather_v(r):
        j, k = sl[r], share[r]
        V.tensor_copy(T.hb[:, 1024 * j:1024 * j + 16 * k], T.xb[:, 0:1024].indirect(T.off[:, 32 * j:32 * j + k])).then_inc(sem["gv%d" % j], 1)

    def pack_v(r):
        j = sl[r]
        V.wait_ge(sem["gv%d" % j], 1)
        V.wait_ge(sem["gs%d" % j], 2)
        V.quantize_mx(xcol(T.OC, j), xcol(T.OS, j), T.hb[:, 1024 * j:1024 * j + 1024]).then_inc(sem["qz%d" % j], 1)

    whole = [me] + W

    def pick_v(i):
        s = whole[i]
        V.wait_ge(sem["pc%d" % i], 1)
        V.tensor_copy(T.ysb[:, 128 * s:128 * s + 128], T.pf[:, 256 * i:256 * i + 256].indirect(T.offl[:, 8 * i:8 * i + 8])).then_inc(sem["yg%d" % i], 1)

    def full(i, ps, parts):
        for part, (c, p) in enumerate(parts):
            mm = PE.matmul_mx(ps, qcol(T.QC, own), qcol(T.QS, own), c, p, part == 0, part == 1)
        mm.then_inc(sem["pm%d" % i], 1)

    def wparts(f):
        return [(xcol(T.FC, 2 * f + part), xcol(T.FS, 2 * f + part)) for part in range(2)]

    bankA = [T.psA[:, 0:256], T.psA[:, 512:768]]
    bankY = [T.psY[:, 512 * i:512 * i + 256] for i in range(3)]
    PE.wait_ge(sem.qq, 1)
    score("own")
    for j in (2 * fp, 2 * fp + 1):
        PE.wait_ge(sem["q%d" % plan["slots"][j]], 16)
    score("b0f")
    PE.wait_ge(sem["q%d" % plan["slots"][single]], 16)
    PE.wait_ge(sem.snown0, 1)
    PE.wait_ge(sem.snown1, 1)
    score("b0s")
    PE.wait_ge(sem.qr, 1)
    full(0, bankY[2], [(T.XC[:], T.XS[:]), (T.RC[:], T.RS[:])])
    PE.wait_ge(sem.gi, 1)
    turn(0, ["own", "b0f", "b0s"])
    spread(0)
    for r in B:
        PE.wait_ge(sem["q%d" % r], 16)
    score("b1f")
    PE.wait_ge(sem.ofx0, 4)
    turn(1, ["b1f"])
    spread(1)
    for f in range(2):
        PE.wait_ge(sem["w%d0" % f], 16)
        score("w%d" % f)
    PE.wait_ge(sem.pc0, 1)
    PE.wait_ge(sem.w01, 16)
    full(1, bankY[2], wparts(0))
    PE.wait_ge(sem.ofx1, 4)
    turn(2, ["w0", "w1"])
    PE.wait_ge(sem.w11, 16)
    full(2, bankA[0], wparts(1))
    spread(2)

    V.wait_ge(sem.mk, 2)
    V.wait_ge(sem.mtop, 1)
    groups_v("own")
    groups_v("b0f")
    groups_v("b0s")
    V.wait_ge(sem.gp, 2)
    V.wait_ge(sem.ms, 2)
    cells_v(0)
    lists_v(0)
    gather_v(first[0])
    groups_v("b1f")
    pack_v(first[0])
    gather_v(first[1])
    cells_v(1)
    pack_v(first[1])
    gather_v(first[2])
    lists_v(1)
    gather_v(second[0])
    pack_v(first[2])
    gather_v(second[1])
    V.wait_ge(sem.mch, 3)
    V.tensor_scalar(T.chrow[0:1, 0:48], T.off[0:1, 0:192:4], 1.0 / 64.0, None, Op.mult).then_inc(sem.chr, 1)
    pack_v(second[0])
    groups_v("w0")
    groups_v("w1")
    pack_v(second[1])
    V.tensor_scalar(T.offl[:, 0:8], T.off[:, 32 * own:32 * own + 32:4], 0.0, None, Op.add).then_inc(sem.ofx2, 1)
    V.wait_ge(sem.ofx2, 1)
    pick_v(0)
    cells_v(2)
    lists_v(2)
    pick_v(1)
    pick_v(2)

    def keep_s(i, ps):
        S.wait_ge(sem["pm%d" % i], 1)
        S.activation(T.pf[:, 256 * i:256 * i + 256], ps, Copy).then_inc(sem["pc%d" % i], 1)

    for b in range(4):
        S.wait_ge(sem["rs%d" % b], 1)
    keep_s(0, bankY[2])
    S.wait_ge(sem.ofx0, 4)
    for r in first:
        gather_s(r)
    S.wait_ge(sem.ofx1, 4)
    for r in second:
        gather_s(r)
    keep_s(1, bankY[2])
    keep_s(2, bankA[0])

    sent = [0]

    def tr(src, dsts, mask, rsem):
        ids = []
        for c, ap in dsts:
            rid, pid = topo.addr(c, core)
            ids.append(DstId(rid=rid, pnc=pid))
        sent[0] += count(mask)
        return RemoteDMATransfer(dst_ids=ids, dma_engine_mask=mask, remote_sem=rsem, srcs=[src], dsts=[ap for c, ap in dsts])

    def post(*transfers):
        g.remote_dma_fused(list(transfers), local_sem=sem.sent)

    far = topo.mask(core, cores[P[0]])
    for r in P + [M] + X:
        far &= topo.mask(core, cores[r])
    near = topo.mask(core, relays[0]) & topo.mask(core, relays[1]) & ~far

    g.iota(T.p16[:], [[0, 8], [1, 16]], 0, 0, allow_small_or_imprecise_dtypes=True).then_inc(sem.gp, 1)
    g.iota(T.pcol[:], [[0, 8]], 0, 1, allow_small_or_imprecise_dtypes=True).then_inc(sem.gp, 1)
    g.wait_ge(sem.mo, 1)
    g.affine_select(T.eb[:], T.ob[:], [[-1, 528]], Op.is_equal, 0.0, 4, 4).then_inc(sem.ge, 1)

    g.wait_ge(sem.qq, 1)
    qsem = sem["q%d" % me]
    for ranks in (P, B):
        at = [(cores[r], plans[r]["slots"].index(me)) for r in ranks]
        post(tr(qcol(T.QC, own).bitcast(u8), [(c, qcol(T.QC, j).bitcast(u8)) for c, j in at], far, qsem))
        post(tr(qcol(T.QS, own), [(c, qcol(T.QS, j)) for c, j in at], far, qsem))

    g.wait_ge(sem.mf, 1)
    g.affine_select(T.idn[:], T.onf[:], [[-1, 128]], Op.is_equal, 0.0, 0, 1).then_inc(sem.gi, 1)

    for part, (c, p, ready) in enumerate(((T.XC, T.XS, sem.qx), (T.RC, T.RS, sem.qr))):
        g.wait_ge(ready, 1)
        post(tr(c[:].bitcast(u8), [(h, xcol(T.HFC, part).bitcast(u8)) for h in relays], near, sem["hfc%d" % part]))
        post(tr(p[:], [(h, xcol(T.HFS, part)) for h in relays], near, sem["hfs%d" % part]))
    g.affine_select(T.m24[:], T.onf[:, 0:24], [[0, 3], [-1, 8]], Op.is_equal, 0.0, 0, 1).then_inc(sem.gm, 1)

    def send_chosen(r):
        j = sl[r]
        g.wait_ge(sem["qz%d" % j], 1)
        if r in plan["x_relay"]:
            h = relays[plan["x_relay"][r]]
            post(tr(xcol(T.OC, j).bitcast(u8), [(h, T.HXC[:].bitcast(u8))], near, sem.hxc))
            post(tr(xcol(T.OS, j), [(h, T.HXS[:])], near, sem.hxs))
        else:
            k = plans[r]["slots"].index(me)
            post(tr(xcol(T.OC, j).bitcast(u8), [(cores[r], xcol(T.LC, k).bitcast(u8))], far, sem["d%d" % me]))
            post(tr(xcol(T.OS, j), [(cores[r], xcol(T.LS, k))], far, sem["d%d" % me]))

    for r in chosen_ranks[:-1]:
        send_chosen(r)
    one = 1 << topo.engines(core, cores[M])[0]
    g.wait_ge(sem.chs, 16)
    post(tr(T.chd[:], [(cores[r], T.chland[me]) for r in chosen_ranks], one, sem.chi))
    send_chosen(chosen_ranks[-1])
    g.wait_ge(sem.sent, sent[0])

    ybank = [T.psY[:, 0:128], T.psY[:, 512:640], T.psA[:, 512:640], T.psY[:, 1024:1152], T.psA[:, 0:128]]
    for i, s in enumerate(plan["yorder"]):
        j = sl[s]
        PE.wait_ge(sem["d%d" % s], 16)
        if i >= 3:
            PE.wait_ge(sem["pc%d" % (i - 2)], 1)
        for part in range(2):
            a = 256 * j + 128 * part
            mm = PE.matmul_mx(ybank[i], qcol(T.QC, own), qcol(T.QS, own), T.LC[:, a:a + 128], T.LS[:, a:a + 128], part == 0, part == 1)
        mm.then_inc(sem["ym%d" % j], 1)
        S.wait_ge(sem["ym%d" % j], 1)
        S.activation(T.ysb[:, 128 * s:128 * s + 128], ybank[i], Copy).then_inc(sem["yc%d" % j], 1)
        S.wait_ge(sem["yc%d" % j], 1)
        S.dma_start(T.y[:, 128 * s:128 * s + 128], T.ysb[:, 128 * s:128 * s + 128]).then_inc(sem.yd, 16)
    S.wait_ge(sem.yd, 16 * len(plan["yorder"]))

    SY.wait_ge(sem.chr, 1)
    SY.dma_start(T.chd[:], T.chrow[0:1, :]).then_inc(sem.chs, 16)

    def store_sy(i):
        s = whole[i]
        SY.wait_ge(sem["yg%d" % i], 1)
        SY.dma_start(T.y[:, 128 * s:128 * s + 128], T.ysb[:, 128 * s:128 * s + 128]).then_inc(sem.ye, 16)

    store_sy(0)
    SY.wait_ge(sem.chi, len(chosen_ranks))
    SY.wait_ge(sem.mch, 3)
    for s in chosen_ranks:
        a = 8 * plans[s]["slots"].index(me)
        SY.dma_start(T.chc[s:s + 1, 0:8], T.chland[s:s + 1, a:a + 8, 0]).then_inc(sem.chg, 16)
    store_sy(1)
    store_sy(2)
    V.tensor_scalar(T.chk[0:8, :], T.offl[0:8, 0:24], T.pcol[0:8, 0:1], 1.0 / 16.0, Op.subtract, Op.mult).then_inc(sem.chv, 1)
    V.wait_ge(sem.chv, 1)
    V.wait_ge(sem.gm, 1)
    V.tensor_tensor(T.chm[0:8, :], T.chk[0:8, :], T.m24[0:8, :], Op.mult).then_inc(sem.chv, 1)
    V.wait_ge(sem.chv, 2)
    for i, s in enumerate(whole):
        V.tensor_reduce(T.chl[0:8, s:s + 1], T.chm[0:8, 8 * i:8 * i + 8], AxisListType.X, Op.add).then_inc(sem.chl1, 1)
    V.wait_ge(sem.chg, 16 * len(chosen_ranks))
    V.transpose(T.cht[0:32, :], T.chc[0:32, :]).then_inc(sem.chv, 1)
    V.wait_ge(sem.chv, 3)
    V.wait_ge(sem.chl1, len(whole))
    V.tensor_tensor(T.chf[0:8, :], T.cht[0:8, 0:8], T.chl[0:8, :], Op.add).then_inc(sem.chf1, 1)
    SY.wait_ge(sem.chf1, 1)
    SY.dma_start(T.ch[:], T.chf[0:8, :]).then_inc(sem.cho, 16)
    SY.wait_ge(sem.cho, 16)
    SY.wait_ge(sem.ye, 16 * len(whole))


def relay_program(g, core, me, T, topo):
    plan = make_plan(me, T, topo)
    if core not in plan["relays"]:
        return
    cores, sem = T.cores, T.sem
    which = plan["relays"].index(core)
    home = cores[me]
    near = topo.mask(home, core) & ~topo.mask(home, cores[plan["P"][0]])
    arrive = count(near)
    u8 = dt.uint8
    sent = [0]

    def send(wait, dst, out, src, rsem):
        g.wait_ge(wait, arrive)
        rid, pid = topo.addr(dst, core)
        mask = topo.mask(core, dst)
        sent[0] += count(mask)
        g.remote_dma_fused([RemoteDMATransfer(dst_ids=[DstId(rid=rid, pnc=pid)], dma_engine_mask=mask, remote_sem=rsem,
                                              srcs=[src], dsts=[out])], local_sem=sem.sent)

    for r, i in plan["w_relay"].items():
        if i == which:
            f = make_plan(r, T, topo)["W"].index(me)
            for part in range(2):
                a, k = 256 * part, 512 * f + 256 * part
                there = sem["w%d%d" % (f, part)]
                send(sem["hfc%d" % part], cores[r], T.FC[:, k:k + 256].bitcast(u8), T.HFC[:, a:a + 256].bitcast(u8), there)
                send(sem["hfs%d" % part], cores[r], T.FS[:, k:k + 256], T.HFS[:, a:a + 256], there)
    for r, i in plan["x_relay"].items():
        if i == which:
            k = 256 * make_plan(r, T, topo)["slots"].index(me)
            there = sem["d%d" % me]
            send(sem.hxc, cores[r], T.LC[:, k:k + 256].bitcast(u8), T.HXC[:].bitcast(u8), there)
            send(sem.hxs, cores[r], T.LS[:, k:k + 256], T.HXS[:], there)
    g.wait_ge(sem.sent, sent[0])
